import numpy as np, ml_dtypes
CORES = [3,7,11,15,131,135,139,143]
N = 8
import mx_ref
BF = ml_dtypes.bfloat16
def gentries(a):
    return np.ascontiguousarray(a.reshape(8, 16, -1).transpose(0, 2, 1)).reshape(8, -1)
def gtable(e):
    e = np.asarray(e); return np.ascontiguousarray(e.reshape(8, -1, 16).transpose(0, 2, 1)).reshape(128, -1).astype(np.int32)
def gcols(t, e):
    v = np.concatenate([t.reshape(8, 16, -1, 4), np.zeros((8, 16, 1, 4), BF)], axis=2)
    return np.ascontiguousarray(np.stack([v[g][:, e[g]] for g in range(8)])).reshape(128, -1)
def tile(rs):
    return np.stack(rs, axis=2).reshape(128, -1).astype(BF)
def pick(q, e):
    c = np.concatenate([q[0].reshape(128, -1, 4), np.zeros((128, 1, 4), np.uint8)], axis=1); s = np.concatenate([q[1], np.ones((16, 1), np.uint8)], axis=1)
    return (np.ascontiguousarray(c[:, e].reshape(128, -1)), np.ascontiguousarray(s[:, e]))
def join(*qs):
    return (np.concatenate([q[0] for q in qs], axis=1), np.concatenate([q[1] for q in qs], axis=1))
def put(q, e, v):
    c, s = q[0].reshape(128, -1, 4).copy(), q[1].copy(); c[:, e] = v[0].reshape(128, -1, 4); s[:, e] = v[1]
    return (c.reshape(128, -1), s)
def pk(c, s):
    return (np.ascontiguousarray(c), mx_ref.live(s))
def emit(q):
    return q[0], q[1]
def packed(v, rng):
    q = [mx_ref.quantize(np.ascontiguousarray(v[r])) for r in range(N)]
    return np.stack([a for a, b in q]), np.stack([mx_ref.plane(b, rng) for a, b in q])
def values_of_codes():
    e, c = np.zeros((128, 128, 4), np.float32), np.zeros((128, 2, 4), np.uint8)
    e[np.arange(128), np.arange(128), 0] = 1
    c[:127, :, 0] = np.arange(256).reshape(2, 128).T[:127]
    return mx_ref.matmul(mx_ref.quantize(e.reshape(128, 512).astype(BF)), (c.reshape(128, 8), np.full((16, 2), 127, np.uint8))).T.reshape(-1).astype(np.float64)
CODE_VALUE, SCALE_VALUE = values_of_codes(), 2.0 ** (np.arange(256) - 127.0)
def decode(q):
    return (CODE_VALUE[q[0]].reshape(16, 8, -1, 4) * SCALE_VALUE[q[1]][:, None, :, None] + 0.0).reshape(128, -1).astype(np.float32)
def f(rng, *shape):
    return mx_ref.flush((rng.standard_normal(shape, dtype=np.float32) * np.exp2(rng.integers(-2, 3, shape[:-1] + (1,)))).astype(BF))
def wide(rng, *shape, cols=0):
    v = rng.standard_normal(shape, dtype=np.float32) * np.exp2(rng.integers(-12, 13, shape)).astype(np.float32)
    if cols: v *= np.repeat(np.exp2(rng.integers(-cols, cols + 1, shape[:-2] + (1, shape[-1] // 4))) * (rng.random(shape[:-2] + (1, shape[-1] // 4)) > 0.0625), 4, axis=-1).astype(np.float32)
    return mx_ref.flush(v.astype(BF))
C, H = 288, 144
STEP = [4, 1, 2]
def numbers_of(rng):
    return {"x": np.array(f(rng, N, 128, 4 * C)), "u": np.array(f(rng, N, 128, 512)), "v": np.array(f(rng, N, 128, 512))}
def lists(rng):
    e = np.tile(np.arange(C), (N, 8, 1))
    q = rng.permuted(e, axis=2)
    p = np.zeros((N, 8, C), np.int64)
    np.put_along_axis(p, q, np.ascontiguousarray(q.reshape(N, 8, H, 2)[..., ::-1]).reshape(N, 8, C), axis=2)
    return rng.permuted(e, axis=2), p
def stored(n, p):
    return {k: np.stack([gtable(e[r]) for r in range(N)]) for k, e in (("nx", n), ("iv", np.argsort(n, axis=2)), ("pr", p))}
def layer(rng, still=[]):
    w = np.array(f(rng, 128, 2048)).reshape(8, 16, 4, 8, 16, 4)
    for i in still:
        w[:, i] = 0
        w[:, :, :, :, i] = 0
    return w
def weights(rng, w):
    c, s = packed(np.stack([np.ascontiguousarray(w).reshape(128, 2048)] * N), rng)
    return {"wc": c, "ws": s}
def setup_inputs(rng):
    return {**numbers_of(rng), **stored(*lists(rng)), **weights(rng, layer(rng))}
def setup_inputs_ties(rng):
    d = numbers_of(rng)
    n, p = lists(rng)
    o = rng.permutation(N)
    k = rng.integers(-1, 2, (N, 8, C))
    k[o[1]] = 1
    k[o[2]] = 1
    t = rng.integers(0, 2, (8, C))
    t = np.where(np.arange(C) < p[o[3]], t, 1 - np.take_along_axis(t, p[o[3]], axis=1))
    k[o[3]] = np.where(t == 1, 1, rng.integers(-1, 1, (8, C)))
    a = np.exp2(rng.integers(-3, 4, (8, 1)).astype(np.float32))
    x = d["x"].reshape(N, 8, 16, C, 4)
    x[:, :, 0] = 0
    x[:, :, 0, :, 0] = k.astype(np.float32).astype(BF)
    x[:, :, 8:] = 0
    x[:, :, 8, :, 0] = (-1.125 * a).astype(BF)
    x[:, :, 10, :, 0] = (-0.0703125 * a).astype(BF)
    u = d["u"].reshape(N, 128, 128, 4)
    u[:, :, ::16] = 0
    for r in range(N):
        for h in range(0, 128, 16): u[r, h, h, 0] = 0.0 if r == o[0] else -1.0 if r == o[2] else 1.0
    w = layer(rng, [0])
    w[:, :, :, :, 8:] = 0
    for g in range(8):
        w[g, 8, 0, g, 8, 0] = -28.0
        for b in range(4): w[g, 10, b, g, 9, 0] = -2.0 ** (b - 5)
    return {"x": x.reshape(N, 128, 4 * C), "u": u.reshape(N, 128, 512), "v": d["v"], **stored(n, p), **weights(rng, w)}
def setup_inputs_near(rng):
    d = numbers_of(rng)
    k = np.where(rng.permutation(N) % 2 == 0, 2.0 ** -30, 1.0)
    x = rng.choice([-1.0, 1.0], (N, 8, 16, C, 4)) * (1.0 + 0.125 * rng.integers(0, 8, (N, 8, 16, C, 4))) * 64.0 * k[:, None, None, None, None]
    x[:, :, :9] = 0
    s = rng.integers(-1, 2, (N, 8, C)) * k[:, None, None]
    x[:, :, 0, :, 0] = 1.125 * s
    x[:, :, 1, :, 0] = -1.25 * s
    x[:, :, 7, :, 0] = k[:, None, None]
    x[:, :, 8, :, 0] = rng.choice([-1.0, 1.0], (N, 8, C)) * k[:, None, None]
    x[:, :, 9, :, 0] = 64.0 * k[:, None, None]
    for r in range(N):
        at = [0, C - 1, int(rng.integers(C)), int(rng.integers(C))]
        for g, j in zip(rng.permutation(8)[:4], at): x[r, g, 0, j, 0] = 2.0 ** 30 * rng.choice([-1.0, 1.0])
    u = d["u"].reshape(N, 128, 128, 4)
    u[:, :, ::16] = 0
    for h in range(0, 128, 16):
        u[:, h, h, 0] = (1.125 * k).astype(np.float32).astype(BF)
        u[:, h + 1, h, 0] = k.astype(np.float32).astype(BF)
        u[:, h + 2, h, 0] = k.astype(np.float32).astype(BF)
    w = layer(rng, list(range(10)))
    for g in range(8):
        w[g, 8, 0, g, 2, 0] = 2.0 ** -8
        w[g, 9, 0, g, 7, 0] = 1.0
    return {"x": x.astype(np.float32).reshape(N, 128, 4 * C).astype(BF), "u": u.reshape(N, 128, 512), "v": d["v"], **stored(*lists(rng)), **weights(rng, w)}
def setup_inputs_odd(rng):
    d = numbers_of(rng)
    x = (1.0 + (2 * rng.integers(0, 64, (N, 16, 8, C, 4)) + 1) * 2.0 ** -7) * np.exp2(-rng.integers(0, 7, (N, 16, 8, C, 4)).astype(np.float64)) * rng.choice([-1.0, 1.0], (N, 16, 8, C, 4))
    x[:, :, 0, :, 0] = rng.choice([1.96875, 1.875], (N, 16, C)) * 2.0 ** 8 * rng.choice([-1.0, 1.0], (N, 16, C))
    k = np.exp2(rng.integers(0, 4, (N, 8, C)) - 5.0)
    r = int(rng.integers(N))
    k[r] = k[r, :1].copy()
    x[:, ::2, 1, :, 0] = k * (1.0 + 0.125 * rng.integers(0, 2, (N, 8, C)))
    x[:, ::2, 2, :, 0] = k
    x[r, 0, 1, :, 0] = k[r, 0]
    u = d["u"].reshape(N, 16, 8, 128, 4)
    u[:, :, :, ::16] = 0
    for g in range(8):
        u[:, 2 * g, 1, 16 * g, 0] = 1.0
        u[:, 2 * g, 2, 16 * g, 0] = -1.0
    for g, i, e in ((0, 1, 4), (3, 2, 2)):
        u[r, :, :, 16 * g] = 0
        u[r, 0, i, 16 * g, 0] = 1.0
        u[r, 2 * e, 1, 16 * g, 0] = 1.875 * 2.0 ** -25
        u[r, 14, 2, 16 * g, 0] = -1.0
    return {"x": x.astype(np.float32).reshape(N, 128, 4 * C).astype(BF), "u": u.reshape(N, 128, 512), "v": d["v"], **stored(*lists(rng)), **weights(rng, layer(rng, [0, 1, 2, 8]))}
def setup_inputs_ends(rng):
    d = numbers_of(rng)
    o, e = rng.permutation(N) % 4, rng.permutation(N) % 4
    c = rng.choice([-1.0, 1.0], (N, C))
    c[:, H:] = -c[:, :H][:, ::-1]
    s = rng.choice([-1.0, 1.0], (N, 128, C, 4))
    s[o == 0] = -1
    s[o == 1] = c[o == 1][:, None, :, None]
    s[o == 3] = s[o == 3][:, :, :1]
    x = s * (0.63 + 0.06 * rng.random((N, 128, C, 4))) * 2.0 ** 30
    x[o == 3] = s[o == 3] * 2.0 ** -26
    x[o == 3, 48:64] = s[o == 3, 48:64] * 2.0 ** -30
    x[:, 120:] = s[:, 120:] * 2.0 ** -29
    a = np.stack([rng.permutation(8) % 2 * 2.0 - 1.0 for r in range(N)]) * np.where(o < 2, 2.0 ** 30, 2.0 ** -30)[:, None]
    u = d["u"].reshape(N, 128, 128, 4)
    u[:, :, ::16] = a.astype(np.float32).astype(BF)[:, None, :, None]
    v = rng.choice([-1.0, 1.0], (N, 128, 512)) * np.where(o % 2 == 0, 2.0 ** 30, 2.0 ** -30)[:, None, None]
    n, p = lists(rng)
    i = np.arange(C)
    p[o == 0] = i ^ 1
    p[o == 1] = C - 1 - i
    p[o == 2] = (i + H) % C
    n[e == 0] = i
    n[e == 1] = C - 1 - i
    n[e == 2] = (i + 1) % C
    n[e == 3] = p[e == 3]
    w = np.zeros((128, 4, 128, 4), np.float32)
    j = np.arange(128)
    for b in range(4): w[j, b, j, b] = np.where(j // 16 == 3, 0.0, np.where(j < 120, -4.0, 256.0))
    return {"x": x.astype(np.float32).reshape(N, 128, 4 * C).astype(BF), "u": u.reshape(N, 128, 512), "v": v.astype(np.float32).astype(BF), **stored(n, p), **weights(rng, w.astype(BF))}
def setup_inputs_spread(rng):
    d = setup_inputs(rng)
    d["x"] = wide(rng, N, 128, 4 * C, cols=6)
    return d
def check_inputs(d):
    b = []
    for k in ("x", "u", "v"):
        a = np.abs(d[k].astype(np.float32))
        if not (np.isfinite(a).all() and ((a == 0) | (a >= 2.0 ** -30) & (a <= 2.0 ** 30)).all()): b.append("a value of " + k)
    none, least, most = [emit(mx_ref.quantize(np.full((128, 16), k, np.float32).astype(BF)))[1][0, 0] for k in (0.0, 2.0 ** -8, 2.0 ** 8)]
    full = np.arange(C)
    for k in ("nx", "iv", "pr"):
        if not ((d[k] >= 0) & (d[k] < C)).all(): b.append("an entry of " + k)
    for r in range(N):
        n, i, p = [np.clip(gentries(d[k][r]), 0, C - 1) for k in ("nx", "iv", "pr")]
        if not (np.take_along_axis(i, n, axis=1) == full).all(): b.append("iv: not the inverse of nx")
        if not (np.take_along_axis(p, p, axis=1) == full).all() or (p == full).any(): b.append("pr: not pairs")
        if ((d["wc"][r] == 0x7F) | (d["wc"][r] == 0xFF)).any(): b.append("wc: a code that is no number")
        s = mx_ref.live(d["ws"][r])
        if ((s != none) & ((s < least) | (s > most))).any(): b.append("ws: a scale out of range")
        if (((d["wc"][r].reshape(16, 8, 512, 4) & 0x7F) != 0) & (s == none)[:, None, :, None]).any(): b.append("wc: a code other than zero under the scale of zeros")
        if (d["wc"][r] != d["wc"][0]).any() or (s != mx_ref.live(d["ws"][0])).any(): b.append("wc and ws: not the same on all ranks")
    return b
def reference(x, u, v, nx, iv, pr, wc, ws):
    qu = [mx_ref.quantize(u[r]) for r in range(N)]
    lay = [[pick(pk(wc[r], ws[r]), np.arange(128 * b, 128 * b + 128)) for b in range(4)] for r in range(N)]
    nxt, inv, pair = [[gentries(t[r]).astype(np.int64) for r in range(N)] for t in (nx, iv, pr)]
    now = [x[r] for r in range(N)]
    for step in STEP:
        had, made = [], []
        for r in range(N):
            n, m = nxt[r], inv[r]
            q = mx_ref.quantize(now[r])
            had.append(decode(q).astype(BF))
            bit = mx_ref.matmul(qu[r], q)[::16] > 0
            t = np.where(bit == np.take_along_axis(bit, pair[r], axis=1), pair[r], np.arange(C))
            for g in (0, 2, 4, 6, 1, 3, 5, 7):
                h = (g + 1) % 8
                w = n[g][t[g][m[g]]]
                n[g], m[g] = n[g][t[g]], t[g][m[g]]
                n[h], m[h] = n[h][w], w[m[h]]
            one = gcols(had[r], n).astype(np.float32)
            two = gcols(had[r], np.take_along_axis(n, n, axis=1)).astype(np.float32)
            z = mx_ref.quantize(((one + two) * np.float32(0.5)).astype(BF))
            made.append(mx_ref.quantize(tile([mx_ref.matmul(lay[r][b], z) * np.float32(0.03125) for b in range(4)])))
        for r in range(N):
            k = decode(join(pick(made[r], np.arange(H)), pick(made[r ^ step], np.arange(H, C)))).astype(BF)
            now[r] = (had[r].astype(np.float32) + gcols(k, inv[r]).astype(np.float32)).astype(BF)
    y, nl = np.zeros((N, 128, C), np.float32), np.zeros((N, 8, C), np.float32)
    oc, osc = np.zeros((N, 128, 4 * C), np.uint8), np.zeros((N, 16, C), np.uint8)
    for r in range(N):
        q = mx_ref.quantize(now[r])
        y[r] = mx_ref.matmul(mx_ref.quantize(v[r]), q)
        nl[r] = nxt[r]
        oc[r], osc[r] = emit(q)
    return {"y": y, "nl": nl, "oc": oc, "osc": osc}

@@ -1,0 +1,490 @@
+from concourse.mybir import dt, AluOpType, ActivationFunctionType
+
+ALU = AluOpType
+ACT = ActivationFunctionType
+C, HC, NT = 288, 144, 18
+STEP = [4, 1, 2]
+F32, BF, U16, I32, CODE, U8 = "float32", "bfloat16", "uint16", "int32", "float8_e4m3fn_x4", "uint8"
+SCRATCH = {}
+PART = {}
+
+
+def _b(w, dtype, *names):
+    for n in names:
+        SCRATCH[n] = ("sbuf", [128, w], dtype)
+
+
+def _v(buf, w, dtype, *names):
+    _b(w * len(names), dtype, buf)
+    for i, n in enumerate(names):
+        PART[n] = (buf, w * i, w)
+
+
+_b(4 * C, BF, "xin", "xtl", "zt")
+_b(512, BF, "uin", "vin")
+_b(516, BF, "half", "ebase")
+_b(576, BF, "hta", "htb")
+_b(C, BF, "fp0", "fp1", "fp2", "fp3", "gp0", "gp1", "gp2", "gp3", "xp0", "xp1", "xp2", "xp3", "gc0", "gc1", "gc2", "gc3")
+_b(C, BF, "sg1", "sg3", "sh1", "sh3", "ag1", "ag3", "sc1", "sc3", "cs2")
+_b(C, F32, "iot", "nval", "fa", "fb", "al", "be", "cm", "scn", "nlb", "yb")
+_b(2 * C, F32, "w1", "mv2")
+_v("tbl", NT, F32, "idt", "id2", "ido", "tbs", "lpe", "tt0", "s1s", "dif", "d2e", "d2o", "x2e", "x2f", "k0", "k1", "k2", "k3", "k4", "k5")
+_b(36, F32, "d34", "x34", "t34")
+_b(54, F32, "e0", "oo0", "e1", "oo1", "dst1")
+_b(72, F32, "dst2")
+_b(90, F32, "own")
+_b(54, I32, "l0", "l1")
+_b(NT, I32, "lp")
+_v("icol", 1, I32, "pix", "pq", "po")
+_v("fcol", 1, F32, "qc", "od", "ev", "nod", "bc", "nbc", "kc", "c0", "c1", "od288")
+_b(16, F32, "pcs", "pcm", "uof")
+_v("run", 16, F32, "i16", "dfq", "p0", "p1", "p2")
+_b(NT, U16, "noff", "moff", "pb1", "pb3", "taf", "tbf", "mx0", "nof0", "o1", "o2", "o3", "o4", "a1", "qof")
+_b(8, U16, "uo1", "uo3")
+for _n, _w in (("qx", C), ("wq", 512), ("eq0", 128), ("eq1", 128), ("eq2", 128), ("eq3", 128), ("qu", 128), ("u1", 128), ("u3", 128), ("qv", 128),
+               ("qz0", C), ("qz1", C), ("qz2", C), ("zl0", HC), ("zl1", HC), ("zl2", HC), ("qha", HC), ("qhb", HC)):
+    _b(_w, CODE, _n)
+    _b(_w, U8, _n + "s")
+for _n in range(8):
+    SCRATCH["ps%d" % _n] = ("psum", [128, 512], F32)
+SEMAPHORES = ["kV", "kS", "kT", "kG", "loc", "arr0", "arr1", "arr2"] + ["d%d" % _i for _i in range(40)]
+
+
+def rank_program(g, core, T, topo):
+    rank = T.rank_of(core)
+    if rank is None:
+        return
+    queues = {"V": g.vector, "S": g.scalar, "T": g.tensor, "G": g, "Y": g.sync}
+    known = {q: {} for q in queues}
+    clock = {}
+    count = {}
+    log = {}
+
+    def wait(q, tok):
+        if known[q].get(tok[0], 0) >= tok[1]:
+            return
+        queues[q].wait_ge(T.sem[tok[0]], tok[1])
+        for s, v in clock[tok].items():
+            known[q][s] = max(known[q].get(s, 0), v)
+
+    def reg(name, a=0, b=None, step=1, p=0, n=128):
+        name, o, w = PART.get(name, (name, 0, SCRATCH.get(name, (0, (0, 0)))[1][1]))
+        return (name, o + a, o + (w if b is None else b), step, p, n)
+
+    def view(r):
+        name, a, b, step, p, n = r
+        if p == 0 and n == 128:
+            return T[name][:, a:b] if step == 1 else T[name][:, a:b:step]
+        return T[name][p:p + n, a:b] if step == 1 else T[name][p:p + n, a:b:step]
+
+    def meet(x, y):
+        if x[1] >= y[2] or y[1] >= x[2] or x[4] >= y[4] + y[5] or y[4] >= x[4] + x[5]:
+            return False
+        return not (x[3] == y[3] and x[3] > 1 and (x[1] - y[1]) % x[3])
+
+    def order(q, reads, writes):
+        need = {}
+        for r, w in [(r, False) for r in reads] + [(r, True) for r in writes]:
+            bank = SCRATCH[r[0]][0] == "psum"
+            for r2, tok, q2, w2 in log.get(r[0], []):
+                if (w or w2) and meet(r, r2) or bank and q2 != q:
+                    need[tok[0]] = max(need.get(tok[0], 0), tok[1])
+        for s in sorted(need, key=lambda s: -need[s]):
+            wait(q, (s, need[s]))
+
+    def note(q, tok, reads, writes):
+        clock[tok] = dict(known[q])
+        clock[tok][tok[0]] = tok[1]
+        for r in writes:
+            log[r[0]] = [e for e in log.get(r[0], []) if e[0] != r]
+        for r, w in [(r, False) for r in reads] + [(r, True) for r in writes]:
+            log.setdefault(r[0], []).append((r, tok, q, w))
+
+    def op(q, make, reads, writes):
+        order(q, reads, writes)
+        s = "k" + q
+        count[s] = count.get(s, 0) + 1
+        make().then_inc(T.sem[s], 1)
+        note(q, (s, count[s]), reads, writes)
+
+    nd = [0]
+
+    def dmas(q, items):
+        s = "d%d" % nd[0]
+        nd[0] += 1
+        tot = 16 * len(items)
+        for o, i, rd, wr in items:
+            order(q, rd, wr)
+            queues[q].dma_start(o, i).then_inc(T.sem[s], 16)
+        count[s] = tot
+        for o, i, rd, wr in items:
+            note(q, (s, tot), rd, wr)
+        clock[(s, tot)] = dict(known[q])
+        clock[(s, tot)][s] = tot
+
+    def load(name, src, p=0, n=128, a=0, b=None):
+        r = reg(name, a, b, 1, p, n)
+        return (view(r), src, [], [r])
+
+    def ts(o, i, s1, s2, f0, f1=None, ind=None):
+        rd = [i] + [reg(s) for s in (s1, s2) if isinstance(s, str)] + ([ind] if ind else [])
+        x1, x2 = [view(reg(s)) if isinstance(s, str) else s for s in (s1, s2)]
+        src = view(i).indirect(view(ind)) if ind else view(i)
+        if f1 is None:
+            op("V", lambda: g.vector.tensor_scalar(view(o), src, x1, None, f0), rd, [o])
+        else:
+            op("V", lambda: g.vector.tensor_scalar(view(o), src, x1, x2, f0, f1), rd, [o])
+
+    def tt(o, i0, i1, f, ind=None):
+        src = view(i0).indirect(view(ind)) if ind else view(i0)
+        op("V", lambda: g.vector.tensor_tensor(view(o), src, view(i1), f), [i0, i1] + ([ind] if ind else []), [o])
+
+    def vcopy(o, i, ind=None):
+        src = view(i).indirect(view(ind)) if ind else view(i)
+        op("V", lambda: g.vector.tensor_copy(view(o), src), [i] + ([ind] if ind else []), [o])
+
+    def scopy(o, i, ind=None, scale=1.0):
+        src = view(i).indirect(view(ind)) if ind else view(i)
+        op("S", lambda: g.scalar.activation(view(o), src, ACT.Copy, scale=scale), [i] + ([ind] if ind else []), [o])
+
+    def gather(q, o, i, ind):
+        (vcopy if q == "V" else scopy)(o, i, ind)
+
+    def scan(o, d0, d1, init, f1):
+        op("V", lambda: g.vector.tensor_tensor_scan(view(o), view(d0), view(d1), init, ALU.max, f1), [d0, d1], [o])
+
+    def quant(code, src, a=0, b=None):
+        ro, rs = reg(code, a, b), reg(code + "s", a, b)
+        op("V", lambda: g.vector.quantize_mx(view(ro), view(rs), view(src)), [src], [ro, rs])
+
+    def mm(bank, n, st, sa, mv, ma):
+        l, ls, r, rs = reg(st, sa, sa + 128), reg(st + "s", sa, sa + 128), reg(mv, ma, ma + n), reg(mv + "s", ma, ma + n)
+        o = reg("ps%d" % bank, 0, n)
+        op("T", lambda: g.tensor.matmul_mx(view(o), view(l), view(ls), view(r), view(rs), True, True), [l, ls, r, rs], [o])
+
+    def iota(r, pattern, base, cm, whole=False):
+        if whole:
+            op("G", lambda: g.iota(view(r), pattern, base, cm), [], [r])
+        else:
+            op("G", lambda: g.iota(view(r), pattern, base, cm, allow_small_or_imprecise_dtypes=True), [], [r])
+
+    def fill(r, v):
+        op("V", lambda: g.vector.memset(view(r), v), [], [r])
+
+    def table(o, sc):
+        ts(o, reg(sc, 15, C, 16), 1024.0, -1.0, ALU.mult, ALU.add)
+
+    def own_table(slot, src, between=None):
+        scan(reg("scn"), src, reg("cm"), 0.0, ALU.mult)
+        if between:
+            between()
+        table(slot, "scn")
+
+    AL, BE, GA = reg("own", 0, 18), reg("own", 18, 36), reg("own", 36, 54)
+    OM, ON = reg("own", 54, 72), reg("own", 72, 90)
+    N_, M_ = reg("l0", 0, 18), reg("l0", 18, 36)
+    W0, W1 = reg("w1", 0, 2 * C, 2), reg("w1", 1, 2 * C, 2)
+
+    def shift():
+        it = []
+        for h in range(8):
+            a = 18 * (h % 2)
+            o, i = reg("dst1", 0, 54, 1, 16 * h, 16), reg("own", a, a + 54, 1, 16 * ((h + 7) % 8), 16)
+            it.append((view(o), view(i), [i], [o]))
+        for h in range(0, 8, 2):
+            o, i = reg("dst2", 0, 72, 1, 16 * h, 16), reg("own", 18, 90, 1, 16 * ((h + 6) % 8), 16)
+            it.append((view(o), view(i), [i], [o]))
+        dmas("Y", it)
+
+    def selects():
+        s0, s1, s2 = reg("dst1", 0, 18), reg("dst1", 18, 36), reg("dst1", 36, 54)
+        tt(reg("dif"), s2, s0, ALU.subtract)
+        tt(reg("d34"), reg("dst2", 0, 36), reg("dst2", 36, 72), ALU.subtract)
+        ts(reg("k5"), s1, "ev", None, ALU.mult)
+        ts(reg("k0"), reg("dif"), "kc", None, ALU.mult)
+        ts(reg("t34"), reg("d34"), "nbc", None, ALU.mult)
+        ts(reg("d2e"), reg("dif"), "ev", None, ALU.mult)
+        ts(reg("d2o"), reg("dif"), "nod", None, ALU.mult)
+        tt(reg("x2e"), s0, reg("k0"), ALU.add)
+        tt(reg("x34"), reg("t34"), reg("dst2", 36, 72), ALU.add)
+        tt(reg("a1"), reg("k5"), reg("ido"), ALU.add)
+
+    three = tuple(enumerate((T.nx, T.iv, T.pr)))
+    dmas("Y", [load("l0", v[:], 0, 128, 18 * k, 18 * k + 18) for k, v in three])
+    dmas("S", [load("l1", v[0:112, :], 16, 112, 18 * k, 18 * k + 18) for k, v in three]
+         + [load("l1", v[112:128, :], 0, 16, 18 * k, 18 * k + 18) for k, v in three])
+    dmas("Y", [load("lp", T.pr[16:128, :], 0, 112), load("lp", T.pr[0:16, :], 112, 16)])
+    dmas("Y", [load("xin", T.x[:])])
+    dmas("S", [load("uin", T.u[:])])
+    dmas("Y", [(T.wq[:, 0:512].bitcast(dt.uint8), T.wc[:], [], [reg("wq")]), (T.wqs[:, 0:512], T.ws[:], [], [reg("wqs")])])
+    dmas("Y", [load("vin", T.v[:])])
+
+    iota(reg("pix"), [[0, 1]], 0, 1, True)
+    iota(reg("i16"), [[1, 16]], 0, 0)
+    iota(reg("idt"), [[16, NT]], 0, 0)
+    iota(reg("iot"), [[1, C]], 1, 0)
+    iota(reg("uof", 0, 8), [[32, 4], [0, 2]], 0, 0)
+    iota(reg("uof", 8, 16), [[32, 4], [0, 2]], 16, 0)
+    fill(reg("half"), 0.5)
+    op("G", lambda: g.affine_select(T.ebase[:, :], T.half[:, :], [[-1, 516]], ALU.is_equal, 0.0, 3, 4), [reg("half")], [reg("ebase")])
+    ts(reg("pq"), reg("pix"), 15, None, ALU.bitwise_and)
+    ts(reg("po"), reg("pix"), 4, 1, ALU.arith_shift_right, ALU.bitwise_and)
+    vcopy(reg("qc"), reg("pq"))
+    vcopy(reg("od"), reg("po"))
+    ts(reg("dfq"), reg("i16"), "qc", None, ALU.subtract)
+    ts(reg("p2"), reg("i16"), 15.0, 2.0 ** -20 - 1.0, ALU.is_equal, ALU.mult)
+    ts(reg("ev"), reg("od"), -1.0, 1.0, ALU.mult, ALU.add)
+    ts(reg("qof"), reg("idt"), 0.0, "qc", ALU.mult, ALU.add)
+    ts(reg("p0"), reg("dfq"), 0.0, None, ALU.is_ge)
+    ts(reg("p1"), reg("dfq"), 0.0, 1023.0, ALU.is_equal, ALU.mult)
+    ts(reg("p2"), reg("p2"), 1.0, None, ALU.add)
+    ts(reg("idt"), reg("idt"), "qc", None, ALU.add)
+    tt(reg("p0"), reg("p0"), reg("p1"), ALU.add)
+    ts(reg("tt0"), reg("idt"), "ev", None, ALU.mult)
+    tt(reg("pcm"), reg("p0"), reg("p2"), ALU.mult)
+    fill(reg("mv2"), 0.0)
+    fill(reg("uo3", 0, 1), 112)
+    vcopy(reg("uo1"), reg("uof", 0, 8))
+    vcopy(reg("uo3", 1, 8), reg("uof", 8, 15))
+    gather("S", reg("cm"), reg("pcm"), reg("qof"))
+
+    vcopy(reg("nof0"), N_)
+    ts(reg("e0"), reg("l0"), "ev", None, ALU.mult)
+    ts(reg("oo1"), reg("l1"), "od", None, ALU.mult)
+    tt(reg("mx0"), reg("e0", 18, 36), reg("oo1", 18, 36), ALU.add)
+    tt(reg("taf"), reg("tt0"), reg("oo1", 0, 18), ALU.add)
+    tt(reg("pb1"), reg("e0", 36, 54), reg("oo1", 36, 54), ALU.add)
+    gather("S", reg("nval"), reg("iot"), reg("nof0"))
+    gather("V", reg("mv2", 0, C), reg("iot"), reg("mx0"))
+    ts(reg("lpe"), reg("lp"), "ev", None, ALU.mult)
+    ts(reg("oo0"), reg("l0"), "od", None, ALU.mult)
+    tt(reg("tbf"), reg("lpe"), reg("oo0", 18, 36), ALU.add)
+    gather("S", reg("al"), reg("nval"), reg("taf"))
+    gather("V", reg("be"), reg("mv2"), reg("tbf"))
+    gather("S", W1, reg("al"), reg("pb1"))
+    own_table(AL, reg("al"), lambda: (
+        ts(reg("c0"), reg("qc"), 0.0, -4.0, ALU.is_equal, ALU.mult),
+        ts(reg("p0"), reg("dfq"), 0.0, 2.0, ALU.is_equal, ALU.mult),
+        ts(reg("p1"), reg("dfq"), 0.0, -4.0, ALU.is_lt, ALU.mult),
+        ts(reg("p2"), reg("dfq"), 15.0, -4.0, ALU.is_equal, ALU.mult)))
+    own_table(BE, reg("be"), lambda: (
+        ts(reg("bc"), reg("c0"), 2.0, None, ALU.add),
+        tt(reg("p0"), reg("p0"), reg("p1"), ALU.add),
+        ts(reg("c1"), reg("od"), -2.0, 1.0, ALU.mult, ALU.add),
+        tt(reg("pcs"), reg("p0"), reg("p2"), ALU.add)))
+    for b in range(4):
+        scopy(reg("dst2", 18 * b, 18 * b + 18), reg("idt"))
+    gather("S", reg("cs2"), reg("pcs"), reg("qof"))
+    own_table(GA, W1, lambda: (
+        vcopy(OM, M_),
+        vcopy(ON, N_),
+        ts(reg("id2"), reg("idt"), 2.0, "bc", ALU.mult, ALU.subtract)))
+    shift()
+    scopy(W0, reg("al"))
+
+    def constants():
+        tt(reg("c0"), reg("c1"), reg("bc"), ALU.mult)
+        ts(reg("e1"), reg("l1"), "ev", None, ALU.mult)
+        ts(reg("nbc"), reg("bc"), -1.0, None, ALU.mult)
+        tt(reg("kc"), reg("od"), reg("c0"), ALU.subtract)
+        tt(reg("pb3"), reg("e1", 36, 54), reg("oo0", 36, 54), ALU.add)
+        ts(reg("nod"), reg("od"), -1.0, None, ALU.mult)
+        ts(reg("od288"), reg("od"), 288.0, None, ALU.mult)
+        ts(reg("ido"), reg("idt"), "od", None, ALU.mult)
+        ts(reg("tbs"), reg("lpe"), "od288", None, ALU.add)
+
+    quant("qx", reg("xin", 0, 640), 0, 160)
+    quant("qu", reg("uin"))
+    for o, off in (("u1", "uo1"), ("u3", "uo3")):
+        ro, ri, rf = reg(o), reg("qu"), reg(off)
+        op("V", lambda: g.vector.tensor_copy(view(ro).bitcast(dt.uint32), view(ri).bitcast(dt.uint32).indirect(view(rf))), [ri, rf], [ro])
+        rs, rj = reg(o + "s"), reg("qus")
+        op("S", lambda: g.scalar.activation(view(rs), view(rj).indirect(view(rf)), ACT.Copy), [rj, rf], [rs])
+    quant("qx", reg("xin", 640, 1152), 160, C)
+    for b in range(4):
+        quant("eq%d" % b, reg("ebase", 3 - b, 515 - b))
+
+    use = None
+    for s in STEP:
+        m = topo.mask(core, T.cores[rank ^ s])
+        use = m if use is None else use & m
+    engines = sum(1 for e in range(16) if use >> e & 1)
+
+    def bits(sg, sh, ag, sc, pb):
+        tt(reg(ag), reg(sg), reg(sh), ALU.is_equal, reg(pb))
+        scan(reg(sc), reg(ag), reg("cs2"), -1.0, ALU.add)
+
+    XH = ((0, 160), (160, C))
+    HAND = ("SSVV", "SSSV")
+
+    def both(dst, src, off):
+        for q, (a, b) in zip("VS", XH):
+            gather(q, reg(dst, a, b), reg(src), reg(off, a // 16, b // 16))
+
+    def into_place(k):
+        a, b = XH[k]
+        for p in range(4):
+            o, off = reg("xtl", 4 * a + p, 4 * b, 4), reg("moff", a // 16, b // 16)
+            if HAND[k][p] == "S":
+                scopy(o, reg("xp%d" % p), off, 2.0)
+            else:
+                ts(o, reg("xp%d" % p), 2.0, None, ALU.mult, None, off)
+
+    def layer(src):
+        for b in range(4):
+            mm(4 + b, HC, "wq", 128 * b, src, 0)
+
+    def heights(tile, mine):
+        for b in range(4):
+            o, i = reg(tile, b, 576, 4), reg("ps%d" % (4 + b), 0, HC)
+            if b in mine:
+                ts(o, i, 0.03125, None, ALU.mult)
+            else:
+                scopy(o, i, None, 0.03125)
+
+    def unpack(code, tile):
+        quant(code, reg(tile))
+        for b in range(4):
+            mm(b, HC, "eq%d" % b, 0, code, 0)
+
+    def state(half):
+        a = HC * half
+        for b in range(4):
+            tt(reg("xp%d" % b, a, a + HC), reg("gp%d" % b, a, a + HC), reg("ps%d" % b, 0, HC), ALU.add)
+
+    for r, step in enumerate(STEP):
+        last = r == 2
+        for k, (a, b) in enumerate(XH):
+            if r:
+                quant("qx", reg("xtl", 4 * a, 4 * b), a, b)
+            mm(4 + 2 * k, b - a, "u1", 0, "qx", a)
+            mm(5 + 2 * k, b - a, "u3", 0, "qx", a)
+            if r and not k:
+                into_place(1)
+        for b in range(4):
+            mm(b, C, "eq%d" % b, 0, "qx", 0)
+        if r:
+            selects()
+        for k, sg in ((0, "sg1"), (1, "sg3")):
+            for v, (a, b) in enumerate(XH):
+                o, i = reg(sg, a, b), reg("ps%d" % (4 + 2 * v + k), 0, b - a)
+                op("S", lambda: g.scalar.activation(view(o), view(i), ACT.Sign, bias=-(2.0 ** -93)), [i], [o])
+        for a, b in XH:
+            vcopy(reg("sh1", a, b), reg("sg1", a, b))
+        scopy(reg("sh3"), reg("sg3"))
+        for b in range(2):
+            scopy(reg("fp%d" % b), reg("ps%d" % b, 0, C))
+        s1v, s3v = reg("sc1", 15, C, 16), reg("sc3", 15, C, 16)
+        bits("sg1", "sh1", "ag1", "sc1", "pb1")
+        tt(reg("o1"), s1v, reg("id2"), ALU.add)
+        gather("S", reg("fa"), reg("w1"), reg("o1"))
+        for k in range(4):
+            scopy(reg("s1s", 0, 18, 1, 32 * ((k + 1) % 4), 32), reg("sc1", 15, C, 16, 32 * k, 32))
+        scopy(reg("fp2"), reg("ps2", 0, C))
+        if not r:
+            constants()
+        bits("sg3", "sh3", "ag3", "sc3", "pb3")
+        if not r:
+            selects()
+        tt(reg("k1"), reg("s1s"), reg("d2e"), ALU.mult)
+        tt(reg("k2"), s3v, reg("d2o"), ALU.mult)
+        tt(reg("x2f"), reg("k1"), reg("x2e"), ALU.add)
+        tt(reg("o2"), reg("k2"), reg("x2f"), ALU.add)
+        gather("S", reg("fb"), reg("fa"), reg("o2"))
+        tt(reg("k3"), s3v, reg("d34", 0, 18), ALU.mult)
+        tt(reg("k4"), reg("s1s"), reg("d34", 18, 36), ALU.mult)
+        tt(reg("o3"), reg("k3"), reg("x34", 0, 18), ALU.add)
+        tt(reg("o4"), reg("k4"), reg("x34", 18, 36), ALU.add)
+        both("fa", "fb", "o3")
+        both("fb", "fa", "o4")
+        both("nval", "fb", "a1")
+        scan(reg("scn"), reg("nval"), reg("cm"), 0.0, ALU.mult)
+        scopy(reg("fp3"), reg("ps3", 0, C))
+        table(reg("noff"), "scn")
+        for b in (1, 2, 3):
+            gather("S", reg("gp%d" % b), reg("fp%d" % b), reg("noff"))
+        gather("V", reg("gp0"), reg("fp0"), reg("noff"))
+        qz, zl = "qz%d" % r, "zl%d" % r
+        for bs in ((0, 1), (2, 3)):
+            for b in bs:
+                vcopy(reg("gc%d" % b, 128, C), reg("gp%d" % b, 128, C))
+            for b in bs:
+                tt(reg("zt", 512 + b, 1152, 4), reg("gp%d" % b), reg("gc%d" % b, 128, C), ALU.add, reg("noff", 8, 18))
+        for b in range(4):
+            scopy(reg("gc%d" % b, 0, 128), reg("gp%d" % b, 0, 128))
+        quant(qz, reg("zt", 512, 1152), 128, C)
+        dst = T.cores[rank ^ step]
+        rid, pid = topo.addr(dst, core)
+        zc, zs, arr = reg(qz, HC, C), reg(qz + "s", HC, C), "arr%d" % r
+        order("G", [zc, zs], [])
+        g.remote_dma(T[zl][:, 0:HC].bitcast(dt.uint8), view(zc).bitcast(dt.uint8), T.sem[arr], T.sem.loc, pid, rid, use)
+        g.remote_dma(T[zl + "s"][:, 0:HC], view(zs), T.sem[arr], T.sem.loc, pid, rid, use)
+        count["loc"] = count.get("loc", 0) + 2 * engines
+        count[arr] = 2 * engines
+        clock[(arr, 2 * engines)] = {arr: 2 * engines}
+        for n in (zl, zl + "s"):
+            log[n] = [(reg(n), (arr, 2 * engines), "R", True)]
+        if not last:
+            it = []
+            for h in range(1, 8, 2):
+                o, i = reg("taf", 0, 18, 1, 16 * h, 16), reg("noff", 0, 18, 1, 16 * h - 16, 16)
+                it.append((view(o), view(i), [i], [o]))
+            dmas("Y", it)
+        rm, ri, rf = reg("mv2", 0, C), reg("iot"), reg("noff")
+        op("V", lambda: g.vector.tensor_copy(view(rm).indirect(view(rf)), view(ri)), [ri, rf], [rm])
+        if not last:
+            it = []
+            for h in range(1, 8, 2):
+                o, i = reg("mv2", C, 2 * C, 1, 16 * h, 16), reg("mv2", 0, C, 1, 16 * h - 16, 16)
+                it.append((view(o), view(i), [i], [o]))
+            dmas("Y", it)
+        scan(reg("scn"), rm, reg("cm"), 0.0, ALU.mult)
+        table(reg("moff"), "scn")
+        if not last:
+            table(OM, "scn")
+            ts(reg("k0"), OM, "od", None, ALU.mult)
+            tt(reg("tbf"), reg("k0"), reg("tbs"), ALU.add)
+        for b in range(4):
+            tt(reg("zt", b, 512, 4), reg("gp%d" % b), reg("gc%d" % b, 0, 128), ALU.add, reg("noff", 0, 8))
+        quant(qz, reg("zt", 0, 512), 0, 128)
+        layer(qz)
+        if not last:
+            vcopy(ON, reg("noff"))
+            gather("S", reg("al"), reg("nval"), reg("taf"))
+            gather("S", W1, reg("al"), reg("pb1"))
+            scopy(W0, reg("al"))
+            own_table(AL, reg("al"))
+        else:
+            ts(reg("nlb"), reg("nval"), -1.0, None, ALU.add)
+            quant("qv", reg("vin"))
+            dmas("Y", [(T.nl[h:h + 1, :], view(reg("nlb", 0, C, 1, 16 * h, 1)), [reg("nlb")], []) for h in range(8)])
+        heights("hta", (0,))
+        unpack("qha", "hta")
+        if not last:
+            own_table(GA, W1)
+            gather("S", reg("be"), reg("mv2"), reg("tbf"))
+            own_table(BE, reg("be"))
+            shift()
+        state(0)
+        layer(zl)
+        heights("htb", (0, 2))
+        unpack("qhb", "htb")
+        state(1)
+        into_place(0)
+
+    for k, (a, b) in enumerate(XH):
+        quant("qx", reg("xtl", 4 * a, 4 * b), a, b)
+        mm(4 + k, b - a, "qv", 0, "qx", a)
+        if not k:
+            into_place(1)
+    rc, rs = reg("qx"), reg("qxs")
+    dmas("Y", [(T.oc[:, :], view(rc).bitcast(dt.uint8), [rc], [])])
+    ya, yc = reg("yb", 0, 160), reg("yb", 160, C)
+    scopy(ya, reg("ps4", 0, 160))
+    dmas("S", [(T.y[:, 0:160], view(ya), [ya], [])])
+    vcopy(yc, reg("ps5", 0, 128))
+    dmas("Y", [(T.y[:, 160:C], view(yc), [yc], [])])
+    dmas("Y", [(T.osc[4 * k:4 * k + 4, :], T.qxs[32 * k:32 * k + 4, 0:C], [rs], []) for k in range(4)])
+    for s, v in count.items():
+        if known["G"].get(s, 0) < v:
+            g.wait_ge(T.sem[s], v)

@@ -24,14 +24,14 @@ _b(4 * C, BF, "xin", "xtl", "zt")
 _b(512, BF, "uin", "vin")
 _b(516, BF, "half", "ebase")
 _b(576, BF, "hta", "htb")
-_b(C, BF, "fp0", "fp1", "fp2", "fp3", "gp0", "gp1", "gp2", "gp3", "xp0", "xp1", "xp2", "xp3", "gc0", "gc1", "gc2", "gc3")
+_b(C, BF, "fp0", "fp1", "fp2", "fp3", "gp0", "gp1", "gp2", "gp3", "xp0", "xp1", "xp2", "xp3", "ff0", "ff1", "yp0", "yp1", "gc2", "gc3")
 _b(C, BF, "sg1", "sg3", "sh1", "sh3", "ag1", "ag3", "sc1", "sc3", "cs2")
 _b(C, F32, "iot", "nval", "fa", "fb", "al", "be", "cm", "scn", "nlb", "yb")
 _b(2 * C, F32, "w1", "mv2")
-_v("tbl", NT, F32, "idt", "id2", "ido", "tbs", "lpe", "tt0", "s1s", "dif", "d2e", "d2o", "x2e", "x2f", "k0", "k1", "k2", "k3", "k4", "k5")
-_b(36, F32, "d34", "x34", "t34")
-_b(54, F32, "e0", "oo0", "e1", "oo1", "dst1")
-_b(72, F32, "dst2")
+_v("tbl", NT, F32, "idt", "id2", "ido", "tbs", "lpe", "tt0", "s1s", "dif", "d2e", "d2o", "x2e", "x2f", "k0", "k1", "k2", "k3", "k4")
+_v("t36", 36, F32, "d34", "x34", "t34")
+_v("t54", 54, F32, "e0", "oo0", "e1", "oo1", "see", "seo", "sel")
+_b(72, F32, "dst1", "dst2")
 _b(90, F32, "own")
 _b(54, I32, "l0", "l1")
 _b(NT, I32, "lp")
@@ -126,6 +126,9 @@ def rank_program(g, core, T, topo):
         r = reg(name, a, b, 1, p, n)
         return (view(r), src, [], [r])
 
+    def move(o, i):
+        return (view(o), view(i), [i], [o])
+
     def ts(o, i, s1, s2, f0, f1=None, ind=None):
         rd = [i] + [reg(s) for s in (s1, s2) if isinstance(s, str)] + ([ind] if ind else [])
         x1, x2 = [view(reg(s)) if isinstance(s, str) else s for s in (s1, s2)]
@@ -186,28 +189,21 @@ def rank_program(g, core, T, topo):
     W0, W1 = reg("w1", 0, 2 * C, 2), reg("w1", 1, 2 * C, 2)
 
     def shift():
-        it = []
-        for h in range(8):
-            a = 18 * (h % 2)
-            o, i = reg("dst1", 0, 54, 1, 16 * h, 16), reg("own", a, a + 54, 1, 16 * ((h + 7) % 8), 16)
-            it.append((view(o), view(i), [i], [o]))
-        for h in range(0, 8, 2):
-            o, i = reg("dst2", 0, 72, 1, 16 * h, 16), reg("own", 18, 90, 1, 16 * ((h + 6) % 8), 16)
-            it.append((view(o), view(i), [i], [o]))
-        dmas("Y", it)
+        dmas("Y", [move(reg("dst1", 0, 72, 1, p, n), reg("own", 0, 72, 1, f, n)) for p, f, n in ((16, 0, 112), (0, 112, 16))]
+             + [move(reg("dst2", 0, 72, 1, 16 * h, 16), reg("own", 18, 90, 1, 16 * ((h + 6) % 8), 16)) for h in range(0, 8, 2)])
 
     def selects():
-        s0, s1, s2 = reg("dst1", 0, 18), reg("dst1", 18, 36), reg("dst1", 36, 54)
-        tt(reg("dif"), s2, s0, ALU.subtract)
+        s0, s2 = reg("sel", 0, 18), reg("sel", 36, 54)
+        ts(reg("see"), reg("dst1", 0, 54), "ev", None, ALU.mult)
+        ts(reg("seo"), reg("dst1", 18, 72), "od", None, ALU.mult)
         tt(reg("d34"), reg("dst2", 0, 36), reg("dst2", 36, 72), ALU.subtract)
-        ts(reg("k5"), s1, "ev", None, ALU.mult)
-        ts(reg("k0"), reg("dif"), "kc", None, ALU.mult)
+        tt(reg("a1"), reg("see", 18, 36), reg("ido"), ALU.add)
+        tt(reg("sel"), reg("see"), reg("seo"), ALU.add)
         ts(reg("t34"), reg("d34"), "nbc", None, ALU.mult)
-        ts(reg("d2e"), reg("dif"), "ev", None, ALU.mult)
-        ts(reg("d2o"), reg("dif"), "nod", None, ALU.mult)
-        tt(reg("x2e"), s0, reg("k0"), ALU.add)
+        tt(reg("dif"), s2, s0, ALU.subtract)
         tt(reg("x34"), reg("t34"), reg("dst2", 36, 72), ALU.add)
-        tt(reg("a1"), reg("k5"), reg("ido"), ALU.add)
+        return [lambda: ts(reg("k0"), reg("dif"), "kc", None, ALU.mult), lambda: ts(reg("d2e"), reg("dif"), "ev", None, ALU.mult),
+                lambda: tt(reg("x2e"), s0, reg("k0"), ALU.add), lambda: ts(reg("d2o"), reg("dif"), "nod", None, ALU.mult)]
 
     three = tuple(enumerate((T.nx, T.iv, T.pr)))
     dmas("Y", [load("l0", v[:], 0, 128, 18 * k, 18 * k + 18) for k, v in three])
@@ -246,7 +242,19 @@ def rank_program(g, core, T, topo):
     fill(reg("uo3", 0, 1), 112)
     vcopy(reg("uo1"), reg("uof", 0, 8))
     vcopy(reg("uo3", 1, 8), reg("uof", 8, 15))
+    ts(reg("c0"), reg("qc"), 0.0, -4.0, ALU.is_equal, ALU.mult)
+    ts(reg("c1"), reg("od"), -2.0, 1.0, ALU.mult, ALU.add)
+    ts(reg("nod"), reg("od"), -1.0, None, ALU.mult)
+    ts(reg("bc"), reg("c0"), 1.5, None, ALU.add)
+    ts(reg("od288"), reg("od"), 288.0, None, ALU.mult)
+    ts(reg("ido"), reg("idt"), "od", None, ALU.mult)
+    tt(reg("c1"), reg("c1"), reg("bc"), ALU.mult)
+    ts(reg("nbc"), reg("bc"), -1.0, None, ALU.mult)
+    ts(reg("id2"), reg("idt"), 2.0, "bc", ALU.mult, ALU.subtract)
+    tt(reg("kc"), reg("od"), reg("c1"), ALU.subtract)
     gather("S", reg("cm"), reg("pcm"), reg("qof"))
+    for b in range(4):
+        scopy(reg("dst2", 18 * b, 18 * b + 18), reg("idt"))
 
     vcopy(reg("nof0"), N_)
     ts(reg("e0"), reg("l0"), "ev", None, ALU.mult)
@@ -260,38 +268,25 @@ def rank_program(g, core, T, topo):
     ts(reg("oo0"), reg("l0"), "od", None, ALU.mult)
     tt(reg("tbf"), reg("lpe"), reg("oo0", 18, 36), ALU.add)
     gather("S", reg("al"), reg("nval"), reg("taf"))
-    gather("V", reg("be"), reg("mv2"), reg("tbf"))
     gather("S", W1, reg("al"), reg("pb1"))
+    gather("S", reg("be"), reg("mv2"), reg("tbf"))
     own_table(AL, reg("al"), lambda: (
-        ts(reg("c0"), reg("qc"), 0.0, -4.0, ALU.is_equal, ALU.mult),
         ts(reg("p0"), reg("dfq"), 0.0, 2.0, ALU.is_equal, ALU.mult),
         ts(reg("p1"), reg("dfq"), 0.0, -4.0, ALU.is_lt, ALU.mult),
-        ts(reg("p2"), reg("dfq"), 15.0, -4.0, ALU.is_equal, ALU.mult)))
-    own_table(BE, reg("be"), lambda: (
-        ts(reg("bc"), reg("c0"), 2.0, None, ALU.add),
-        tt(reg("p0"), reg("p0"), reg("p1"), ALU.add),
-        ts(reg("c1"), reg("od"), -2.0, 1.0, ALU.mult, ALU.add),
-        tt(reg("pcs"), reg("p0"), reg("p2"), ALU.add)))
-    for b in range(4):
-        scopy(reg("dst2", 18 * b, 18 * b + 18), reg("idt"))
-    gather("S", reg("cs2"), reg("pcs"), reg("qof"))
+        ts(reg("p2"), reg("dfq"), 15.0, -4.0, ALU.is_equal, ALU.mult),
+        ts(reg("e1"), reg("l1"), "ev", None, ALU.mult)))
     own_table(GA, W1, lambda: (
+        tt(reg("p0"), reg("p0"), reg("p1"), ALU.add),
+        tt(reg("pb3"), reg("e1", 36, 54), reg("oo0", 36, 54), ALU.add),
         vcopy(OM, M_),
+        tt(reg("pcs"), reg("p0"), reg("p2"), ALU.add)))
+    gather("S", reg("cs2"), reg("pcs"), reg("qof"))
+    for b in (2, 3):
+        quant("eq%d" % b, reg("ebase", 3 - b, 515 - b))
+    own_table(BE, reg("be"), lambda: (
         vcopy(ON, N_),
-        ts(reg("id2"), reg("idt"), 2.0, "bc", ALU.mult, ALU.subtract)))
+        ts(reg("tbs"), reg("lpe"), "od288", None, ALU.add)))
     shift()
-    scopy(W0, reg("al"))
-
-    def constants():
-        tt(reg("c0"), reg("c1"), reg("bc"), ALU.mult)
-        ts(reg("e1"), reg("l1"), "ev", None, ALU.mult)
-        ts(reg("nbc"), reg("bc"), -1.0, None, ALU.mult)
-        tt(reg("kc"), reg("od"), reg("c0"), ALU.subtract)
-        tt(reg("pb3"), reg("e1", 36, 54), reg("oo0", 36, 54), ALU.add)
-        ts(reg("nod"), reg("od"), -1.0, None, ALU.mult)
-        ts(reg("od288"), reg("od"), 288.0, None, ALU.mult)
-        ts(reg("ido"), reg("idt"), "od", None, ALU.mult)
-        ts(reg("tbs"), reg("lpe"), "od288", None, ALU.add)
 
     quant("qx", reg("xin", 0, 640), 0, 160)
     quant("qu", reg("uin"))
@@ -301,8 +296,7 @@ def rank_program(g, core, T, topo):
         rs, rj = reg(o + "s"), reg("qus")
         op("S", lambda: g.scalar.activation(view(rs), view(rj).indirect(view(rf)), ACT.Copy), [rj, rf], [rs])
     quant("qx", reg("xin", 640, 1152), 160, C)
-    for b in range(4):
-        quant("eq%d" % b, reg("ebase", 3 - b, 515 - b))
+    scopy(W0, reg("al"))
 
     use = None
     for s in STEP:
@@ -310,8 +304,10 @@ def rank_program(g, core, T, topo):
         use = m if use is None else use & m
     engines = sum(1 for e in range(16) if use >> e & 1)
 
-    def bits(sg, sh, ag, sc, pb):
-        tt(reg(ag), reg(sg), reg(sh), ALU.is_equal, reg(pb))
+    def agree(sg, sh, ag, pb):
+        tt(reg(ag), reg(sg), reg(sh), ALU.mult, reg(pb))
+
+    def table_of(ag, sc):
         scan(reg(sc), reg(ag), reg("cs2"), -1.0, ALU.add)
 
     XH = ((0, 160), (160, C))
@@ -358,60 +354,78 @@ def rank_program(g, core, T, topo):
             if r:
                 quant("qx", reg("xtl", 4 * a, 4 * b), a, b)
             mm(4 + 2 * k, b - a, "u1", 0, "qx", a)
+            mm(k, b - a, "u1", 0, "qx", a)
             mm(5 + 2 * k, b - a, "u3", 0, "qx", a)
             if r and not k:
                 into_place(1)
-        for b in range(4):
+        if not r:
+            for b in (0, 1):
+                quant("eq%d" % b, reg("ebase", 3 - b, 515 - b))
+        rest = selects() if r else []
+        for v, (a, b) in enumerate(XH):
+            ts(reg("sh1", a, b), reg("ps%d" % v, 0, b - a), 0.0, 0.5, ALU.is_gt, ALU.subtract)
+        for b in (2, 3, 0, 1):
             mm(b, C, "eq%d" % b, 0, "qx", 0)
-        if r:
-            selects()
         for k, sg in ((0, "sg1"), (1, "sg3")):
             for v, (a, b) in enumerate(XH):
                 o, i = reg(sg, a, b), reg("ps%d" % (4 + 2 * v + k), 0, b - a)
                 op("S", lambda: g.scalar.activation(view(o), view(i), ACT.Sign, bias=-(2.0 ** -93)), [i], [o])
-        for a, b in XH:
-            vcopy(reg("sh1", a, b), reg("sg1", a, b))
-        scopy(reg("sh3"), reg("sg3"))
-        for b in range(2):
+        scopy(reg("sh3"), reg("sg3"), None, 0.5)
+        for b in (2, 3):
             scopy(reg("fp%d" % b), reg("ps%d" % b, 0, C))
         s1v, s3v = reg("sc1", 15, C, 16), reg("sc3", 15, C, 16)
-        bits("sg1", "sh1", "ag1", "sc1", "pb1")
-        tt(reg("o1"), s1v, reg("id2"), ALU.add)
-        gather("S", reg("fa"), reg("w1"), reg("o1"))
+        agree("sg1", "sh1", "ag1", "pb1")
+        for f in rest[0:1]:
+            f()
+        table_of("ag1", "sc1")
+        for f in rest[1:3]:
+            f()
         for k in range(4):
             scopy(reg("s1s", 0, 18, 1, 32 * ((k + 1) % 4), 32), reg("sc1", 15, C, 16, 32 * k, 32))
-        scopy(reg("fp2"), reg("ps2", 0, C))
+        tt(reg("o1"), s1v, reg("id2"), ALU.add)
+        gather("S", reg("fa"), reg("w1"), reg("o1"))
+        scopy(reg("fp0"), reg("ps0", 0, C))
+        for f in rest[3:]:
+            f()
+        agree("sg3", "sh3", "ag3", "pb3")
         if not r:
-            constants()
-        bits("sg3", "sh3", "ag3", "sc3", "pb3")
-        if not r:
-            selects()
+            for f in selects():
+                f()
         tt(reg("k1"), reg("s1s"), reg("d2e"), ALU.mult)
-        tt(reg("k2"), s3v, reg("d2o"), ALU.mult)
+        table_of("ag3", "sc3")
         tt(reg("x2f"), reg("k1"), reg("x2e"), ALU.add)
-        tt(reg("o2"), reg("k2"), reg("x2f"), ALU.add)
-        gather("S", reg("fb"), reg("fa"), reg("o2"))
+        tt(reg("k2"), s3v, reg("d2o"), ALU.mult)
         tt(reg("k3"), s3v, reg("d34", 0, 18), ALU.mult)
-        tt(reg("k4"), reg("s1s"), reg("d34", 18, 36), ALU.mult)
+        tt(reg("o2"), reg("k2"), reg("x2f"), ALU.add)
+        gather("S", reg("fb", 96, C), reg("fa"), reg("o2", 6, 18))
         tt(reg("o3"), reg("k3"), reg("x34", 0, 18), ALU.add)
-        tt(reg("o4"), reg("k4"), reg("x34", 18, 36), ALU.add)
+        gather("V", reg("fb", 0, 96), reg("fa"), reg("o2", 0, 6))
+        tt(reg("k4"), reg("s1s"), reg("d34", 18, 36), ALU.mult)
+        vcopy(reg("ff0"), reg("fp0"))
         both("fa", "fb", "o3")
+        tt(reg("o4"), reg("k4"), reg("x34", 18, 36), ALU.add)
         both("fb", "fa", "o4")
         both("nval", "fb", "a1")
-        scan(reg("scn"), reg("nval"), reg("cm"), 0.0, ALU.mult)
-        scopy(reg("fp3"), reg("ps3", 0, C))
+        for a, b in XH:
+            scan(reg("scn", a, b), reg("nval", a, b), reg("cm", a, b), 0.0, ALU.mult)
+        scopy(reg("fp1"), reg("ps1", 0, C))
+        vcopy(reg("ff1"), reg("fp1"))
         table(reg("noff"), "scn")
-        for b in (1, 2, 3):
-            gather("S", reg("gp%d" % b), reg("fp%d" % b), reg("noff"))
-        gather("V", reg("gp0"), reg("fp0"), reg("noff"))
         qz, zl = "qz%d" % r, "zl%d" % r
-        for bs in ((0, 1), (2, 3)):
-            for b in bs:
-                vcopy(reg("gc%d" % b, 128, C), reg("gp%d" % b, 128, C))
-            for b in bs:
-                tt(reg("zt", 512 + b, 1152, 4), reg("gp%d" % b), reg("gc%d" % b, 128, C), ALU.add, reg("noff", 8, 18))
-        for b in range(4):
+        for b in (2, 3):
+            gather("S", reg("gp%d" % b), reg("fp%d" % b), reg("noff"))
+        for b in (0, 1):
+            tt(reg("yp%d" % b), reg("fp%d" % b), reg("ff%d" % b), ALU.add, reg("noff"))
+        for b in (0, 1):
+            gather("S", reg("zt", 512 + b, 1152, 4), reg("yp%d" % b), reg("noff", 8, 18))
+        for b in (2, 3):
+            vcopy(reg("gc%d" % b, 128, C), reg("gp%d" % b, 128, C))
+        for b in (2, 3):
+            tt(reg("zt", 512 + b, 1152, 4), reg("gp%d" % b), reg("gc%d" % b, 128, C), ALU.add, reg("noff", 8, 18))
+        for b in (2, 3):
             scopy(reg("gc%d" % b, 0, 128), reg("gp%d" % b, 0, 128))
+        for b in (0, 1):
+            gather("S", reg("zt", b, 512, 4), reg("yp%d" % b), reg("noff", 0, 8))
         quant(qz, reg("zt", 512, 1152), 128, C)
         dst = T.cores[rank ^ step]
         rid, pid = topo.addr(dst, core)
@@ -425,26 +439,18 @@ def rank_program(g, core, T, topo):
         for n in (zl, zl + "s"):
             log[n] = [(reg(n), (arr, 2 * engines), "R", True)]
         if not last:
-            it = []
-            for h in range(1, 8, 2):
-                o, i = reg("taf", 0, 18, 1, 16 * h, 16), reg("noff", 0, 18, 1, 16 * h - 16, 16)
-                it.append((view(o), view(i), [i], [o]))
-            dmas("Y", it)
+            dmas("Y", [move(reg("taf", 0, 18, 1, 16 * h, 16), reg("noff", 0, 18, 1, 16 * h - 16, 16)) for h in range(1, 8, 2)])
         rm, ri, rf = reg("mv2", 0, C), reg("iot"), reg("noff")
         op("V", lambda: g.vector.tensor_copy(view(rm).indirect(view(rf)), view(ri)), [ri, rf], [rm])
         if not last:
-            it = []
-            for h in range(1, 8, 2):
-                o, i = reg("mv2", C, 2 * C, 1, 16 * h, 16), reg("mv2", 0, C, 1, 16 * h - 16, 16)
-                it.append((view(o), view(i), [i], [o]))
-            dmas("Y", it)
+            dmas("Y", [move(reg("mv2", C, 2 * C, 1, 16 * h, 16), reg("mv2", 0, C, 1, 16 * h - 16, 16)) for h in range(1, 8, 2)])
         scan(reg("scn"), rm, reg("cm"), 0.0, ALU.mult)
         table(reg("moff"), "scn")
         if not last:
             table(OM, "scn")
             ts(reg("k0"), OM, "od", None, ALU.mult)
             tt(reg("tbf"), reg("k0"), reg("tbs"), ALU.add)
-        for b in range(4):
+        for b in (2, 3):
             tt(reg("zt", b, 512, 4), reg("gp%d" % b), reg("gc%d" % b, 0, 128), ALU.add, reg("noff", 0, 8))
         quant(qz, reg("zt", 0, 512), 0, 128)
         layer(qz)
@@ -454,7 +460,9 @@ def rank_program(g, core, T, topo):
             gather("S", W1, reg("al"), reg("pb1"))
             scopy(W0, reg("al"))
             own_table(AL, reg("al"))
-        else:
+        for b in (0, 1):
+            gather("S", reg("gp%d" % b), reg("fp%d" % b), reg("noff"))
+        if last:
             ts(reg("nlb"), reg("nval"), -1.0, None, ALU.add)
             quant("qv", reg("vin"))
             dmas("Y", [(T.nl[h:h + 1, :], view(reg("nlb", 0, C, 1, 16 * h, 1)), [reg("nlb")], []) for h in range(8)])
@@ -474,11 +482,12 @@ def rank_program(g, core, T, topo):
 
     for k, (a, b) in enumerate(XH):
         quant("qx", reg("xtl", 4 * a, 4 * b), a, b)
+        rc = reg("qx", a, b)
+        dmas("Y", [(T.oc[:, 4 * a:4 * b], view(rc).bitcast(dt.uint8), [rc], [])])
         mm(4 + k, b - a, "qv", 0, "qx", a)
         if not k:
             into_place(1)
-    rc, rs = reg("qx"), reg("qxs")
-    dmas("Y", [(T.oc[:, :], view(rc).bitcast(dt.uint8), [rc], [])])
+    rs = reg("qxs")
     ya, yc = reg("yb", 0, 160), reg("yb", 160, C)
     scopy(ya, reg("ps4", 0, 160))
     dmas("S", [(T.y[:, 0:160], view(ya), [ya], [])])

@@ -25,18 +25,18 @@ _b(512, BF, "uin", "vin")
 _b(516, BF, "half", "ebase")
 _b(576, BF, "hta", "htb")
 _b(C, BF, "fp0", "fp1", "fp2", "fp3", "gp0", "gp1", "gp2", "gp3", "xp0", "xp1", "xp2", "xp3", "ff0", "ff1", "yp0", "yp1", "gc2", "gc3")
-_b(C, BF, "sg1", "sg3", "sh1", "sh3", "ag1", "ag3", "sc1", "sc3", "cs2")
+_b(C, BF, "sg1", "sg3", "sp1", "sp3", "sa1", "sa3", "sc1", "sc3", "cs2")
 _b(C, F32, "iot", "nval", "fa", "fb", "al", "be", "cm", "scn", "nlb", "yb")
 _b(2 * C, F32, "w1", "mv2")
-_v("tbl", NT, F32, "idt", "id2", "ido", "tbs", "lpe", "tt0", "s1s", "dif", "d2e", "d2o", "x2e", "x2f", "k0", "k1", "k2", "k3", "k4")
-_v("t36", 36, F32, "d34", "x34", "t34")
-_v("t54", 54, F32, "e0", "oo0", "e1", "oo1", "see", "seo", "sel")
+_v("tbl", NT, F32, "idt", "id2", "ido", "tbs", "lpe", "tt0", "s1", "s3", "s1s", "dif", "d2e", "d2o", "x2e", "x2f", "k0", "k1", "k2", "k3", "k4")
+_v("t36", 36, F32, "d34")
+_v("t54", 54, F32, "e0", "oo0", "e1", "oo1", "see", "seo")
 _b(72, F32, "dst1", "dst2")
 _b(90, F32, "own")
 _b(54, I32, "l0", "l1")
 _b(NT, I32, "lp")
 _v("icol", 1, I32, "pix", "pq", "po")
-_v("fcol", 1, F32, "qc", "od", "ev", "nod", "bc", "nbc", "kc", "c0", "c1", "od288")
+_v("fcol", 1, F32, "qc", "od", "ev", "od288")
 _b(16, F32, "pcs", "pcm", "uof")
 _v("run", 16, F32, "i16", "dfq", "p0", "p1", "p2")
 _b(NT, U16, "noff", "moff", "pb1", "pb3", "taf", "tbf", "mx0", "nof0", "o1", "o2", "o3", "o4", "a1", "qof")
@@ -150,6 +150,9 @@ def rank_program(g, core, T, topo):
         src = view(i).indirect(view(ind)) if ind else view(i)
         op("S", lambda: g.scalar.activation(view(o), src, ACT.Copy, scale=scale), [i] + ([ind] if ind else []), [o])
 
+    def gcopy(o, i):
+        op("G", lambda: g.affine_select(view(o), view(i), [[0, i[2] - i[1]]], ALU.is_gt, 0.0, 1, 0), [i], [o])
+
     def gather(q, o, i, ind):
         (vcopy if q == "V" else scopy)(o, i, ind)
 
@@ -193,17 +196,17 @@ def rank_program(g, core, T, topo):
              + [move(reg("dst2", 0, 72, 1, 16 * h, 16), reg("own", 18, 90, 1, 16 * ((h + 6) % 8), 16)) for h in range(0, 8, 2)])
 
     def selects():
-        s0, s2 = reg("sel", 0, 18), reg("sel", 36, 54)
         ts(reg("see"), reg("dst1", 0, 54), "ev", None, ALU.mult)
         ts(reg("seo"), reg("dst1", 18, 72), "od", None, ALU.mult)
         tt(reg("d34"), reg("dst2", 0, 36), reg("dst2", 36, 72), ALU.subtract)
+        tt(reg("k0"), reg("see", 36, 54), reg("seo", 0, 18), ALU.add)
+        tt(reg("x2e"), reg("see", 0, 18), reg("seo", 36, 54), ALU.add)
         tt(reg("a1"), reg("see", 18, 36), reg("ido"), ALU.add)
-        tt(reg("sel"), reg("see"), reg("seo"), ALU.add)
-        ts(reg("t34"), reg("d34"), "nbc", None, ALU.mult)
-        tt(reg("dif"), s2, s0, ALU.subtract)
-        tt(reg("x34"), reg("t34"), reg("dst2", 36, 72), ALU.add)
-        return [lambda: ts(reg("k0"), reg("dif"), "kc", None, ALU.mult), lambda: ts(reg("d2e"), reg("dif"), "ev", None, ALU.mult),
-                lambda: tt(reg("x2e"), s0, reg("k0"), ALU.add), lambda: ts(reg("d2o"), reg("dif"), "nod", None, ALU.mult)]
+        tt(reg("dif"), reg("k0"), reg("x2e"), ALU.subtract)
+
+    def masks():
+        ts(reg("d2e"), reg("dif"), "ev", None, ALU.mult)
+        ts(reg("d2o"), reg("dif"), "od", None, ALU.mult)
 
     three = tuple(enumerate((T.nx, T.iv, T.pr)))
     dmas("Y", [load("l0", v[:], 0, 128, 18 * k, 18 * k + 18) for k, v in three])
@@ -242,17 +245,15 @@ def rank_program(g, core, T, topo):
     fill(reg("uo3", 0, 1), 112)
     vcopy(reg("uo1"), reg("uof", 0, 8))
     vcopy(reg("uo3", 1, 8), reg("uof", 8, 15))
-    ts(reg("c0"), reg("qc"), 0.0, -4.0, ALU.is_equal, ALU.mult)
-    ts(reg("c1"), reg("od"), -2.0, 1.0, ALU.mult, ALU.add)
-    ts(reg("nod"), reg("od"), -1.0, None, ALU.mult)
-    ts(reg("bc"), reg("c0"), 1.5, None, ALU.add)
     ts(reg("od288"), reg("od"), 288.0, None, ALU.mult)
     ts(reg("ido"), reg("idt"), "od", None, ALU.mult)
-    tt(reg("c1"), reg("c1"), reg("bc"), ALU.mult)
-    ts(reg("nbc"), reg("bc"), -1.0, None, ALU.mult)
-    ts(reg("id2"), reg("idt"), 2.0, "bc", ALU.mult, ALU.subtract)
-    tt(reg("kc"), reg("od"), reg("c1"), ALU.subtract)
+    ts(reg("id2"), reg("idt"), 2.0, None, ALU.mult)
     gather("S", reg("cm"), reg("pcm"), reg("qof"))
+    ts(reg("p0"), reg("dfq"), 0.0, 2.0, ALU.is_equal, ALU.mult)
+    ts(reg("p1"), reg("dfq"), 0.0, -4.0, ALU.is_lt, ALU.mult)
+    ts(reg("p2"), reg("dfq"), 15.0, -4.0, ALU.is_equal, ALU.mult)
+    tt(reg("p0"), reg("p0"), reg("p1"), ALU.add)
+    tt(reg("pcs"), reg("p0"), reg("p2"), ALU.add)
     for b in range(4):
         scopy(reg("dst2", 18 * b, 18 * b + 18), reg("idt"))
 
@@ -270,33 +271,25 @@ def rank_program(g, core, T, topo):
     gather("S", reg("al"), reg("nval"), reg("taf"))
     gather("S", W1, reg("al"), reg("pb1"))
     gather("S", reg("be"), reg("mv2"), reg("tbf"))
-    own_table(AL, reg("al"), lambda: (
-        ts(reg("p0"), reg("dfq"), 0.0, 2.0, ALU.is_equal, ALU.mult),
-        ts(reg("p1"), reg("dfq"), 0.0, -4.0, ALU.is_lt, ALU.mult),
-        ts(reg("p2"), reg("dfq"), 15.0, -4.0, ALU.is_equal, ALU.mult),
-        ts(reg("e1"), reg("l1"), "ev", None, ALU.mult)))
-    own_table(GA, W1, lambda: (
-        tt(reg("p0"), reg("p0"), reg("p1"), ALU.add),
-        tt(reg("pb3"), reg("e1", 36, 54), reg("oo0", 36, 54), ALU.add),
-        vcopy(OM, M_),
-        tt(reg("pcs"), reg("p0"), reg("p2"), ALU.add)))
     gather("S", reg("cs2"), reg("pcs"), reg("qof"))
-    for b in (2, 3):
-        quant("eq%d" % b, reg("ebase", 3 - b, 515 - b))
-    own_table(BE, reg("be"), lambda: (
-        vcopy(ON, N_),
-        ts(reg("tbs"), reg("lpe"), "od288", None, ALU.add)))
+    scopy(W0, reg("al"))
+    own_table(AL, reg("al"), lambda: (
+        ts(reg("e1"), reg("l1"), "ev", None, ALU.mult),
+        vcopy(OM, M_)))
+    own_table(GA, W1, lambda: (
+        tt(reg("pb3"), reg("e1", 36, 54), reg("oo0", 36, 54), ALU.add),
+        vcopy(ON, N_)))
+    own_table(BE, reg("be"), lambda: ts(reg("tbs"), reg("lpe"), "od288", None, ALU.add))
     shift()
 
     quant("qx", reg("xin", 0, 640), 0, 160)
     quant("qu", reg("uin"))
+    quant("qx", reg("xin", 640, 1152), 160, C)
     for o, off in (("u1", "uo1"), ("u3", "uo3")):
         ro, ri, rf = reg(o), reg("qu"), reg(off)
         op("V", lambda: g.vector.tensor_copy(view(ro).bitcast(dt.uint32), view(ri).bitcast(dt.uint32).indirect(view(rf))), [ri, rf], [ro])
         rs, rj = reg(o + "s"), reg("qus")
         op("S", lambda: g.scalar.activation(view(rs), view(rj).indirect(view(rf)), ACT.Copy), [rj, rf], [rs])
-    quant("qx", reg("xin", 640, 1152), 160, C)
-    scopy(W0, reg("al"))
 
     use = None
     for s in STEP:
@@ -304,11 +297,8 @@ def rank_program(g, core, T, topo):
         use = m if use is None else use & m
     engines = sum(1 for e in range(16) if use >> e & 1)
 
-    def agree(sg, sh, ag, pb):
-        tt(reg(ag), reg(sg), reg(sh), ALU.mult, reg(pb))
-
-    def table_of(ag, sc):
-        scan(reg(sc), reg(ag), reg("cs2"), -1.0, ALU.add)
+    def table_of(sc, sg):
+        scan(reg(sc), reg(sg), reg("cs2"), -1.0, ALU.add)
 
     XH = ((0, 160), (160, C))
     HAND = ("SSVV", "SSSV")
@@ -343,10 +333,16 @@ def rank_program(g, core, T, topo):
         for b in range(4):
             mm(b, HC, "eq%d" % b, 0, code, 0)
 
-    def state(half):
+    def state(half, planes):
         a = HC * half
-        for b in range(4):
+        for b in planes:
             tt(reg("xp%d" % b, a, a + HC), reg("gp%d" % b, a, a + HC), reg("ps%d" % b, 0, HC), ALU.add)
+
+    def by_list(b):
+        gather("S", reg("gp%d" % b), reg("fp%d" % b), reg("noff"))
+
+    def mean(b, z, a, e):
+        tt(reg("zt", 4 * z + b, 4 * (z + e - a), 4), reg("gp%d" % b), reg("gc%d" % b, a, e), ALU.add, reg("noff", a // 16, e // 16))
 
     for r, step in enumerate(STEP):
         last = r == 2
@@ -354,66 +350,62 @@ def rank_program(g, core, T, topo):
             if r:
                 quant("qx", reg("xtl", 4 * a, 4 * b), a, b)
             mm(4 + 2 * k, b - a, "u1", 0, "qx", a)
-            mm(k, b - a, "u1", 0, "qx", a)
             mm(5 + 2 * k, b - a, "u3", 0, "qx", a)
             if r and not k:
                 into_place(1)
         if not r:
-            for b in (0, 1):
+            for b in range(4):
                 quant("eq%d" % b, reg("ebase", 3 - b, 515 - b))
-        rest = selects() if r else []
-        for v, (a, b) in enumerate(XH):
-            ts(reg("sh1", a, b), reg("ps%d" % v, 0, b - a), 0.0, 0.5, ALU.is_gt, ALU.subtract)
-        for b in (2, 3, 0, 1):
+        for b in range(4):
             mm(b, C, "eq%d" % b, 0, "qx", 0)
-        for k, sg in ((0, "sg1"), (1, "sg3")):
-            for v, (a, b) in enumerate(XH):
+        if r:
+            selects()
+        for v, (a, b) in enumerate(XH):
+            for k, sg in ((0, "sg1"), (1, "sg3")):
                 o, i = reg(sg, a, b), reg("ps%d" % (4 + 2 * v + k), 0, b - a)
                 op("S", lambda: g.scalar.activation(view(o), view(i), ACT.Sign, bias=-(2.0 ** -93)), [i], [o])
-        scopy(reg("sh3"), reg("sg3"), None, 0.5)
-        for b in (2, 3):
-            scopy(reg("fp%d" % b), reg("ps%d" % b, 0, C))
-        s1v, s3v = reg("sc1", 15, C, 16), reg("sc3", 15, C, 16)
-        agree("sg1", "sh1", "ag1", "pb1")
-        for f in rest[0:1]:
-            f()
-        table_of("ag1", "sc1")
-        for f in rest[1:3]:
-            f()
+        both("sp1", "sg1", "pb1")
+        gather("S", reg("sp3"), reg("sg3"), reg("pb3"))
+        table_of("sa1", "sg1")
+        table_of("sc1", "sp1")
+        if r:
+            masks()
+        tt(reg("s1"), reg("sa1", 15, C, 16), reg("sc1", 15, C, 16), ALU.is_equal)
+        table_of("sa3", "sg3")
         for k in range(4):
-            scopy(reg("s1s", 0, 18, 1, 32 * ((k + 1) % 4), 32), reg("sc1", 15, C, 16, 32 * k, 32))
-        tt(reg("o1"), s1v, reg("id2"), ALU.add)
+            scopy(reg("s1s", 0, 18, 1, 32 * ((k + 1) % 4), 32), reg("s1", 0, 18, 1, 32 * k, 32))
+        tt(reg("o1"), reg("s1"), reg("id2"), ALU.add)
         gather("S", reg("fa"), reg("w1"), reg("o1"))
-        scopy(reg("fp0"), reg("ps0", 0, C))
-        for f in rest[3:]:
-            f()
-        agree("sg3", "sh3", "ag3", "pb3")
+        (vcopy if r else scopy)(reg("fp0"), reg("ps0", 0, C))
+        gcopy(reg("ff0"), reg("fp0"))
         if not r:
-            for f in selects():
-                f()
+            selects()
+            masks()
+        table_of("sc3", "sp3")
         tt(reg("k1"), reg("s1s"), reg("d2e"), ALU.mult)
-        table_of("ag3", "sc3")
+        tt(reg("s3"), reg("sa3", 15, C, 16), reg("sc3", 15, C, 16), ALU.is_equal)
         tt(reg("x2f"), reg("k1"), reg("x2e"), ALU.add)
-        tt(reg("k2"), s3v, reg("d2o"), ALU.mult)
-        tt(reg("k3"), s3v, reg("d34", 0, 18), ALU.mult)
+        tt(reg("k2"), reg("s3"), reg("d2o"), ALU.mult)
+        tt(reg("k3"), reg("s3"), reg("d34", 0, 18), ALU.mult)
         tt(reg("o2"), reg("k2"), reg("x2f"), ALU.add)
         gather("S", reg("fb", 96, C), reg("fa"), reg("o2", 6, 18))
-        tt(reg("o3"), reg("k3"), reg("x34", 0, 18), ALU.add)
+        tt(reg("o3"), reg("k3"), reg("dst2", 36, 54), ALU.add)
         gather("V", reg("fb", 0, 96), reg("fa"), reg("o2", 0, 6))
         tt(reg("k4"), reg("s1s"), reg("d34", 18, 36), ALU.mult)
-        vcopy(reg("ff0"), reg("fp0"))
+        vcopy(reg("fp1"), reg("ps1", 0, C))
         both("fa", "fb", "o3")
-        tt(reg("o4"), reg("k4"), reg("x34", 18, 36), ALU.add)
+        tt(reg("o4"), reg("k4"), reg("dst2", 54, 72), ALU.add)
+        gcopy(reg("ff1"), reg("fp1"))
         both("fb", "fa", "o4")
         both("nval", "fb", "a1")
         for a, b in XH:
             scan(reg("scn", a, b), reg("nval", a, b), reg("cm", a, b), 0.0, ALU.mult)
-        scopy(reg("fp1"), reg("ps1", 0, C))
-        vcopy(reg("ff1"), reg("fp1"))
+        for b in (2, 3):
+            scopy(reg("fp%d" % b), reg("ps%d" % b, 0, C))
         table(reg("noff"), "scn")
         qz, zl = "qz%d" % r, "zl%d" % r
         for b in (2, 3):
-            gather("S", reg("gp%d" % b), reg("fp%d" % b), reg("noff"))
+            by_list(b)
         for b in (0, 1):
             tt(reg("yp%d" % b), reg("fp%d" % b), reg("ff%d" % b), ALU.add, reg("noff"))
         for b in (0, 1):
@@ -421,7 +413,7 @@ def rank_program(g, core, T, topo):
         for b in (2, 3):
             vcopy(reg("gc%d" % b, 128, C), reg("gp%d" % b, 128, C))
         for b in (2, 3):
-            tt(reg("zt", 512 + b, 1152, 4), reg("gp%d" % b), reg("gc%d" % b, 128, C), ALU.add, reg("noff", 8, 18))
+            mean(b, 128, 128, C)
         for b in (2, 3):
             scopy(reg("gc%d" % b, 0, 128), reg("gp%d" % b, 0, 128))
         for b in (0, 1):
@@ -438,46 +430,53 @@ def rank_program(g, core, T, topo):
         clock[(arr, 2 * engines)] = {arr: 2 * engines}
         for n in (zl, zl + "s"):
             log[n] = [(reg(n), (arr, 2 * engines), "R", True)]
+        if last:
+            for s, v in count.items():
+                if s[0] == "d":
+                    wait("G", (s, v))
         if not last:
             dmas("Y", [move(reg("taf", 0, 18, 1, 16 * h, 16), reg("noff", 0, 18, 1, 16 * h - 16, 16)) for h in range(1, 8, 2)])
         rm, ri, rf = reg("mv2", 0, C), reg("iot"), reg("noff")
         op("V", lambda: g.vector.tensor_copy(view(rm).indirect(view(rf)), view(ri)), [ri, rf], [rm])
         if not last:
             dmas("Y", [move(reg("mv2", C, 2 * C, 1, 16 * h, 16), reg("mv2", 0, C, 1, 16 * h - 16, 16)) for h in range(1, 8, 2)])
+        mean(2, 0, 0, 128)
         scan(reg("scn"), rm, reg("cm"), 0.0, ALU.mult)
+        mean(3, 0, 0, 128)
         table(reg("moff"), "scn")
         if not last:
             table(OM, "scn")
-            ts(reg("k0"), OM, "od", None, ALU.mult)
-            tt(reg("tbf"), reg("k0"), reg("tbs"), ALU.add)
-        for b in (2, 3):
-            tt(reg("zt", b, 512, 4), reg("gp%d" % b), reg("gc%d" % b, 0, 128), ALU.add, reg("noff", 0, 8))
         quant(qz, reg("zt", 0, 512), 0, 128)
         layer(qz)
-        if not last:
-            vcopy(ON, reg("noff"))
-            gather("S", reg("al"), reg("nval"), reg("taf"))
-            gather("S", W1, reg("al"), reg("pb1"))
-            scopy(W0, reg("al"))
-            own_table(AL, reg("al"))
-        for b in (0, 1):
-            gather("S", reg("gp%d" % b), reg("fp%d" % b), reg("noff"))
         if last:
+            for b in (0, 1):
+                by_list(b)
             ts(reg("nlb"), reg("nval"), -1.0, None, ALU.add)
             quant("qv", reg("vin"))
             dmas("Y", [(T.nl[h:h + 1, :], view(reg("nlb", 0, C, 1, 16 * h, 1)), [reg("nlb")], []) for h in range(8)])
-        heights("hta", (0,))
-        unpack("qha", "hta")
-        if not last:
-            own_table(GA, W1)
+            heights("hta", (0,))
+            unpack("qha", "hta")
+            state(0, range(4))
+        else:
+            ts(reg("k0"), OM, "od", None, ALU.mult)
+            vcopy(ON, reg("noff"))
+            tt(reg("tbf"), reg("k0"), reg("tbs"), ALU.add)
+            gather("S", reg("al"), reg("nval"), reg("taf"))
+            gather("S", W1, reg("al"), reg("pb1"))
+            by_list(0)
+            own_table(AL, reg("al"), lambda: heights("hta", (0,)))
+            by_list(1)
+            unpack("qha", "hta")
             gather("S", reg("be"), reg("mv2"), reg("tbf"))
-            own_table(BE, reg("be"))
+            own_table(GA, W1, lambda: state(0, (0,)))
+            own_table(BE, reg("be"), lambda: state(0, (1,)))
             shift()
-        state(0)
+            scopy(W0, reg("al"))
+            state(0, (2, 3))
         layer(zl)
         heights("htb", (0, 2))
         unpack("qhb", "htb")
-        state(1)
+        state(1, range(4))
         into_place(0)
 
     for k, (a, b) in enumerate(XH):

from concourse.mybir import dt, AluOpType, ActivationFunctionType

ALU = AluOpType
ACT = ActivationFunctionType
C, HC, NT = 288, 144, 18
STEP = [4, 1, 2]
F32, BF, U16, I32, CODE, U8 = "float32", "bfloat16", "uint16", "int32", "float8_e4m3fn_x4", "uint8"
SCRATCH = {}
PART = {}


def _b(w, dtype, *names):
    for n in names:
        SCRATCH[n] = ("sbuf", [128, w], dtype)


def _v(buf, w, dtype, *names):
    _b(w * len(names), dtype, buf)
    for i, n in enumerate(names):
        PART[n] = (buf, w * i, w)


_b(4 * C, BF, "xin", "xtl", "zt")
_b(512, BF, "uin", "vin")
_b(516, BF, "half", "ebase")
_b(576, BF, "hta", "htb")
_b(C, BF, "fp0", "fp1", "fp2", "fp3", "gp0", "gp1", "gp2", "gp3", "xp0", "xp1", "xp2", "xp3", "ff0", "ff1", "yp0", "yp1", "gc2", "gc3")
_b(C, BF, "sg1", "sg3", "sp1", "sp3", "sa1", "sa3", "sc1", "sc3", "cs2")
_b(C, F32, "iot", "nval", "fa", "fb", "al", "be", "cm", "scn", "nlb", "yb")
_b(2 * C, F32, "w1", "mv2")
_v("tbl", NT, F32, "idt", "id2", "ido", "tbs", "lpe", "tt0", "s1", "s3", "s1s", "dif", "d2e", "d2o", "x2e", "x2f", "k0", "k1", "k2", "k3", "k4")
_v("t36", 36, F32, "d34")
_v("t54", 54, F32, "e0", "oo0", "e1", "oo1", "see", "seo")
_b(72, F32, "dst1", "dst2")
_b(90, F32, "own")
_b(54, I32, "l0", "l1")
_b(NT, I32, "lp")
_v("icol", 1, I32, "pix", "pq", "po")
_v("fcol", 1, F32, "qc", "od", "ev", "od288")
_b(16, F32, "pcs", "pcm", "uof")
_v("run", 16, F32, "i16", "dfq", "p0", "p1", "p2")
_b(NT, U16, "noff", "moff", "pb1", "pb3", "taf", "tbf", "mx0", "nof0", "o1", "o2", "o3", "o4", "a1", "qof")
_b(8, U16, "uo1", "uo3")
for _n, _w in (("qx", C), ("wq", 512), ("eq0", 128), ("eq1", 128), ("eq2", 128), ("eq3", 128), ("qu", 128), ("u1", 128), ("u3", 128), ("qv", 128),
               ("qz0", C), ("qz1", C), ("qz2", C), ("zl0", HC), ("zl1", HC), ("zl2", HC), ("qha", HC), ("qhb", HC)):
    _b(_w, CODE, _n)
    _b(_w, U8, _n + "s")
for _n in range(8):
    SCRATCH["ps%d" % _n] = ("psum", [128, 512], F32)
SEMAPHORES = ["kV", "kS", "kT", "kG", "loc", "arr0", "arr1", "arr2"] + ["d%d" % _i for _i in range(40)]


def rank_program(g, core, T, topo):
    rank = T.rank_of(core)
    if rank is None:
        return
    queues = {"V": g.vector, "S": g.scalar, "T": g.tensor, "G": g, "Y": g.sync}
    known = {q: {} for q in queues}
    clock = {}
    count = {}
    log = {}

    def wait(q, tok):
        if known[q].get(tok[0], 0) >= tok[1]:
            return
        queues[q].wait_ge(T.sem[tok[0]], tok[1])
        for s, v in clock[tok].items():
            known[q][s] = max(known[q].get(s, 0), v)

    def reg(name, a=0, b=None, step=1, p=0, n=128):
        name, o, w = PART.get(name, (name, 0, SCRATCH.get(name, (0, (0, 0)))[1][1]))
        return (name, o + a, o + (w if b is None else b), step, p, n)

    def view(r):
        name, a, b, step, p, n = r
        if p == 0 and n == 128:
            return T[name][:, a:b] if step == 1 else T[name][:, a:b:step]
        return T[name][p:p + n, a:b] if step == 1 else T[name][p:p + n, a:b:step]

    def meet(x, y):
        if x[1] >= y[2] or y[1] >= x[2] or x[4] >= y[4] + y[5] or y[4] >= x[4] + x[5]:
            return False
        return not (x[3] == y[3] and x[3] > 1 and (x[1] - y[1]) % x[3])

    def order(q, reads, writes):
        need = {}
        for r, w in [(r, False) for r in reads] + [(r, True) for r in writes]:
            bank = SCRATCH[r[0]][0] == "psum"
            for r2, tok, q2, w2 in log.get(r[0], []):
                if (w or w2) and meet(r, r2) or bank and q2 != q:
                    need[tok[0]] = max(need.get(tok[0], 0), tok[1])
        for s in sorted(need, key=lambda s: -need[s]):
            wait(q, (s, need[s]))

    def note(q, tok, reads, writes):
        clock[tok] = dict(known[q])
        clock[tok][tok[0]] = tok[1]
        for r in writes:
            log[r[0]] = [e for e in log.get(r[0], []) if e[0] != r]
        for r, w in [(r, False) for r in reads] + [(r, True) for r in writes]:
            log.setdefault(r[0], []).append((r, tok, q, w))

    def op(q, make, reads, writes):
        order(q, reads, writes)
        s = "k" + q
        count[s] = count.get(s, 0) + 1
        make().then_inc(T.sem[s], 1)
        note(q, (s, count[s]), reads, writes)

    nd = [0]

    def dmas(q, items):
        s = "d%d" % nd[0]
        nd[0] += 1
        tot = 16 * len(items)
        for o, i, rd, wr in items:
            order(q, rd, wr)
            queues[q].dma_start(o, i).then_inc(T.sem[s], 16)
        count[s] = tot
        for o, i, rd, wr in items:
            note(q, (s, tot), rd, wr)
        clock[(s, tot)] = dict(known[q])
        clock[(s, tot)][s] = tot

    def load(name, src, p=0, n=128, a=0, b=None):
        r = reg(name, a, b, 1, p, n)
        return (view(r), src, [], [r])

    def move(o, i):
        return (view(o), view(i), [i], [o])

    def ts(o, i, s1, s2, f0, f1=None, ind=None):
        rd = [i] + [reg(s) for s in (s1, s2) if isinstance(s, str)] + ([ind] if ind else [])
        x1, x2 = [view(reg(s)) if isinstance(s, str) else s for s in (s1, s2)]
        src = view(i).indirect(view(ind)) if ind else view(i)
        if f1 is None:
            op("V", lambda: g.vector.tensor_scalar(view(o), src, x1, None, f0), rd, [o])
        else:
            op("V", lambda: g.vector.tensor_scalar(view(o), src, x1, x2, f0, f1), rd, [o])

    def tt(o, i0, i1, f, ind=None):
        src = view(i0).indirect(view(ind)) if ind else view(i0)
        op("V", lambda: g.vector.tensor_tensor(view(o), src, view(i1), f), [i0, i1] + ([ind] if ind else []), [o])

    def vcopy(o, i, ind=None):
        src = view(i).indirect(view(ind)) if ind else view(i)
        op("V", lambda: g.vector.tensor_copy(view(o), src), [i] + ([ind] if ind else []), [o])

    def scopy(o, i, ind=None, scale=1.0):
        src = view(i).indirect(view(ind)) if ind else view(i)
        op("S", lambda: g.scalar.activation(view(o), src, ACT.Copy, scale=scale), [i] + ([ind] if ind else []), [o])

    def gcopy(o, i):
        op("G", lambda: g.affine_select(view(o), view(i), [[0, i[2] - i[1]]], ALU.is_gt, 0.0, 1, 0), [i], [o])

    def gather(q, o, i, ind):
        (vcopy if q == "V" else scopy)(o, i, ind)

    def scan(o, d0, d1, init, f1):
        op("V", lambda: g.vector.tensor_tensor_scan(view(o), view(d0), view(d1), init, ALU.max, f1), [d0, d1], [o])

    def quant(code, src, a=0, b=None):
        ro, rs = reg(code, a, b), reg(code + "s", a, b)
        op("V", lambda: g.vector.quantize_mx(view(ro), view(rs), view(src)), [src], [ro, rs])

    def mm(bank, n, st, sa, mv, ma):
        l, ls, r, rs = reg(st, sa, sa + 128), reg(st + "s", sa, sa + 128), reg(mv, ma, ma + n), reg(mv + "s", ma, ma + n)
        o = reg("ps%d" % bank, 0, n)
        op("T", lambda: g.tensor.matmul_mx(view(o), view(l), view(ls), view(r), view(rs), True, True), [l, ls, r, rs], [o])

    def iota(r, pattern, base, cm, whole=False):
        if whole:
            op("G", lambda: g.iota(view(r), pattern, base, cm), [], [r])
        else:
            op("G", lambda: g.iota(view(r), pattern, base, cm, allow_small_or_imprecise_dtypes=True), [], [r])

    def fill(r, v):
        op("V", lambda: g.vector.memset(view(r), v), [], [r])

    def table(o, sc):
        ts(o, reg(sc, 15, C, 16), 1024.0, -1.0, ALU.mult, ALU.add)

    def own_table(slot, src, between=None):
        scan(reg("scn"), src, reg("cm"), 0.0, ALU.mult)
        if between:
            between()
        table(slot, "scn")

    AL, BE, GA = reg("own", 0, 18), reg("own", 18, 36), reg("own", 36, 54)
    OM, ON = reg("own", 54, 72), reg("own", 72, 90)
    N_, M_ = reg("l0", 0, 18), reg("l0", 18, 36)
    W0, W1 = reg("w1", 0, 2 * C, 2), reg("w1", 1, 2 * C, 2)

    def shift():
        dmas("Y", [move(reg("dst1", 0, 72, 1, p, n), reg("own", 0, 72, 1, f, n)) for p, f, n in ((16, 0, 112), (0, 112, 16))]
             + [move(reg("dst2", 0, 72, 1, 16 * h, 16), reg("own", 18, 90, 1, 16 * ((h + 6) % 8), 16)) for h in range(0, 8, 2)])

    def selects():
        ts(reg("see"), reg("dst1", 0, 54), "ev", None, ALU.mult)
        ts(reg("seo"), reg("dst1", 18, 72), "od", None, ALU.mult)
        tt(reg("d34"), reg("dst2", 0, 36), reg("dst2", 36, 72), ALU.subtract)
        tt(reg("k0"), reg("see", 36, 54), reg("seo", 0, 18), ALU.add)
        tt(reg("x2e"), reg("see", 0, 18), reg("seo", 36, 54), ALU.add)
        tt(reg("a1"), reg("see", 18, 36), reg("ido"), ALU.add)
        tt(reg("dif"), reg("k0"), reg("x2e"), ALU.subtract)

    def masks():
        ts(reg("d2e"), reg("dif"), "ev", None, ALU.mult)
        ts(reg("d2o"), reg("dif"), "od", None, ALU.mult)

    three = tuple(enumerate((T.nx, T.iv, T.pr)))
    dmas("Y", [load("l0", v[:], 0, 128, 18 * k, 18 * k + 18) for k, v in three])
    dmas("S", [load("l1", v[0:112, :], 16, 112, 18 * k, 18 * k + 18) for k, v in three]
         + [load("l1", v[112:128, :], 0, 16, 18 * k, 18 * k + 18) for k, v in three])
    dmas("Y", [load("lp", T.pr[16:128, :], 0, 112), load("lp", T.pr[0:16, :], 112, 16)])
    dmas("Y", [load("xin", T.x[:])])
    dmas("S", [load("uin", T.u[:])])
    dmas("Y", [(T.wq[:, 0:512].bitcast(dt.uint8), T.wc[:], [], [reg("wq")]), (T.wqs[:, 0:512], T.ws[:], [], [reg("wqs")])])
    dmas("Y", [load("vin", T.v[:])])

    iota(reg("pix"), [[0, 1]], 0, 1, True)
    iota(reg("i16"), [[1, 16]], 0, 0)
    iota(reg("idt"), [[16, NT]], 0, 0)
    iota(reg("iot"), [[1, C]], 1, 0)
    iota(reg("uof", 0, 8), [[32, 4], [0, 2]], 0, 0)
    iota(reg("uof", 8, 16), [[32, 4], [0, 2]], 16, 0)
    fill(reg("half"), 0.5)
    op("G", lambda: g.affine_select(T.ebase[:, :], T.half[:, :], [[-1, 516]], ALU.is_equal, 0.0, 3, 4), [reg("half")], [reg("ebase")])
    ts(reg("pq"), reg("pix"), 15, None, ALU.bitwise_and)
    ts(reg("po"), reg("pix"), 4, 1, ALU.arith_shift_right, ALU.bitwise_and)
    vcopy(reg("qc"), reg("pq"))
    vcopy(reg("od"), reg("po"))
    ts(reg("dfq"), reg("i16"), "qc", None, ALU.subtract)
    ts(reg("p2"), reg("i16"), 15.0, 2.0 ** -20 - 1.0, ALU.is_equal, ALU.mult)
    ts(reg("ev"), reg("od"), -1.0, 1.0, ALU.mult, ALU.add)
    ts(reg("qof"), reg("idt"), 0.0, "qc", ALU.mult, ALU.add)
    ts(reg("p0"), reg("dfq"), 0.0, None, ALU.is_ge)
    ts(reg("p1"), reg("dfq"), 0.0, 1023.0, ALU.is_equal, ALU.mult)
    ts(reg("p2"), reg("p2"), 1.0, None, ALU.add)
    ts(reg("idt"), reg("idt"), "qc", None, ALU.add)
    tt(reg("p0"), reg("p0"), reg("p1"), ALU.add)
    ts(reg("tt0"), reg("idt"), "ev", None, ALU.mult)
    tt(reg("pcm"), reg("p0"), reg("p2"), ALU.mult)
    fill(reg("mv2"), 0.0)
    fill(reg("uo3", 0, 1), 112)
    vcopy(reg("uo1"), reg("uof", 0, 8))
    vcopy(reg("uo3", 1, 8), reg("uof", 8, 15))
    ts(reg("od288"), reg("od"), 288.0, None, ALU.mult)
    ts(reg("ido"), reg("idt"), "od", None, ALU.mult)
    ts(reg("id2"), reg("idt"), 2.0, None, ALU.mult)
    gather("S", reg("cm"), reg("pcm"), reg("qof"))
    ts(reg("p0"), reg("dfq"), 0.0, 2.0, ALU.is_equal, ALU.mult)
    ts(reg("p1"), reg("dfq"), 0.0, -4.0, ALU.is_lt, ALU.mult)
    ts(reg("p2"), reg("dfq"), 15.0, -4.0, ALU.is_equal, ALU.mult)
    tt(reg("p0"), reg("p0"), reg("p1"), ALU.add)
    tt(reg("pcs"), reg("p0"), reg("p2"), ALU.add)
    for b in range(4):
        scopy(reg("dst2", 18 * b, 18 * b + 18), reg("idt"))

    vcopy(reg("nof0"), N_)
    ts(reg("e0"), reg("l0"), "ev", None, ALU.mult)
    ts(reg("oo1"), reg("l1"), "od", None, ALU.mult)
    tt(reg("mx0"), reg("e0", 18, 36), reg("oo1", 18, 36), ALU.add)
    tt(reg("taf"), reg("tt0"), reg("oo1", 0, 18), ALU.add)
    tt(reg("pb1"), reg("e0", 36, 54), reg("oo1", 36, 54), ALU.add)
    gather("S", reg("nval"), reg("iot"), reg("nof0"))
    gather("V", reg("mv2", 0, C), reg("iot"), reg("mx0"))
    ts(reg("lpe"), reg("lp"), "ev", None, ALU.mult)
    ts(reg("oo0"), reg("l0"), "od", None, ALU.mult)
    tt(reg("tbf"), reg("lpe"), reg("oo0", 18, 36), ALU.add)
    gather("S", reg("al"), reg("nval"), reg("taf"))
    gather("S", W1, reg("al"), reg("pb1"))
    gather("S", reg("be"), reg("mv2"), reg("tbf"))
    gather("S", reg("cs2"), reg("pcs"), reg("qof"))
    scopy(W0, reg("al"))
    own_table(AL, reg("al"), lambda: (
        ts(reg("e1"), reg("l1"), "ev", None, ALU.mult),
        vcopy(OM, M_)))
    own_table(GA, W1, lambda: (
        tt(reg("pb3"), reg("e1", 36, 54), reg("oo0", 36, 54), ALU.add),
        vcopy(ON, N_)))
    own_table(BE, reg("be"), lambda: ts(reg("tbs"), reg("lpe"), "od288", None, ALU.add))
    shift()

    quant("qx", reg("xin", 0, 640), 0, 160)
    quant("qu", reg("uin"))
    quant("qx", reg("xin", 640, 1152), 160, C)
    for o, off in (("u1", "uo1"), ("u3", "uo3")):
        ro, ri, rf = reg(o), reg("qu"), reg(off)
        op("V", lambda: g.vector.tensor_copy(view(ro).bitcast(dt.uint32), view(ri).bitcast(dt.uint32).indirect(view(rf))), [ri, rf], [ro])
        rs, rj = reg(o + "s"), reg("qus")
        op("S", lambda: g.scalar.activation(view(rs), view(rj).indirect(view(rf)), ACT.Copy), [rj, rf], [rs])

    use = None
    for s in STEP:
        m = topo.mask(core, T.cores[rank ^ s])
        use = m if use is None else use & m
    engines = sum(1 for e in range(16) if use >> e & 1)

    def table_of(sc, sg):
        scan(reg(sc), reg(sg), reg("cs2"), -1.0, ALU.add)

    XH = ((0, 160), (160, C))
    HAND = ("SSVV", "SSSV")

    def both(dst, src, off):
        for q, (a, b) in zip("VS", XH):
            gather(q, reg(dst, a, b), reg(src), reg(off, a // 16, b // 16))

    def into_place(k):
        a, b = XH[k]
        for p in range(4):
            o, off = reg("xtl", 4 * a + p, 4 * b, 4), reg("moff", a // 16, b // 16)
            if HAND[k][p] == "S":
                scopy(o, reg("xp%d" % p), off, 2.0)
            else:
                ts(o, reg("xp%d" % p), 2.0, None, ALU.mult, None, off)

    def layer(src):
        for b in range(4):
            mm(4 + b, HC, "wq", 128 * b, src, 0)

    def heights(tile, mine):
        for b in range(4):
            o, i = reg(tile, b, 576, 4), reg("ps%d" % (4 + b), 0, HC)
            if b in mine:
                ts(o, i, 0.03125, None, ALU.mult)
            else:
                scopy(o, i, None, 0.03125)

    def unpack(code, tile):
        quant(code, reg(tile))
        for b in range(4):
            mm(b, HC, "eq%d" % b, 0, code, 0)

    def state(half, planes):
        a = HC * half
        for b in planes:
            tt(reg("xp%d" % b, a, a + HC), reg("gp%d" % b, a, a + HC), reg("ps%d" % b, 0, HC), ALU.add)

    def by_list(b):
        gather("S", reg("gp%d" % b), reg("fp%d" % b), reg("noff"))

    def mean(b, z, a, e):
        tt(reg("zt", 4 * z + b, 4 * (z + e - a), 4), reg("gp%d" % b), reg("gc%d" % b, a, e), ALU.add, reg("noff", a // 16, e // 16))

    for r, step in enumerate(STEP):
        last = r == 2
        for k, (a, b) in enumerate(XH):
            if r:
                quant("qx", reg("xtl", 4 * a, 4 * b), a, b)
            mm(4 + 2 * k, b - a, "u1", 0, "qx", a)
            mm(5 + 2 * k, b - a, "u3", 0, "qx", a)
            if r and not k:
                into_place(1)
        if not r:
            for b in range(4):
                quant("eq%d" % b, reg("ebase", 3 - b, 515 - b))
        for b in range(4):
            mm(b, C, "eq%d" % b, 0, "qx", 0)
        if r:
            selects()
        for v, (a, b) in enumerate(XH):
            for k, sg in ((0, "sg1"), (1, "sg3")):
                o, i = reg(sg, a, b), reg("ps%d" % (4 + 2 * v + k), 0, b - a)
                op("S", lambda: g.scalar.activation(view(o), view(i), ACT.Sign, bias=-(2.0 ** -93)), [i], [o])
        both("sp1", "sg1", "pb1")
        gather("S", reg("sp3"), reg("sg3"), reg("pb3"))
        table_of("sa1", "sg1")
        table_of("sc1", "sp1")
        if r:
            masks()
        tt(reg("s1"), reg("sa1", 15, C, 16), reg("sc1", 15, C, 16), ALU.is_equal)
        table_of("sa3", "sg3")
        for k in range(4):
            scopy(reg("s1s", 0, 18, 1, 32 * ((k + 1) % 4), 32), reg("s1", 0, 18, 1, 32 * k, 32))
        tt(reg("o1"), reg("s1"), reg("id2"), ALU.add)
        gather("S", reg("fa"), reg("w1"), reg("o1"))
        (vcopy if r else scopy)(reg("fp0"), reg("ps0", 0, C))
        gcopy(reg("ff0"), reg("fp0"))
        if not r:
            selects()
            masks()
        table_of("sc3", "sp3")
        tt(reg("k1"), reg("s1s"), reg("d2e"), ALU.mult)
        tt(reg("s3"), reg("sa3", 15, C, 16), reg("sc3", 15, C, 16), ALU.is_equal)
        tt(reg("x2f"), reg("k1"), reg("x2e"), ALU.add)
        tt(reg("k2"), reg("s3"), reg("d2o"), ALU.mult)
        tt(reg("k3"), reg("s3"), reg("d34", 0, 18), ALU.mult)
        tt(reg("o2"), reg("k2"), reg("x2f"), ALU.add)
        gather("S", reg("fb", 96, C), reg("fa"), reg("o2", 6, 18))
        tt(reg("o3"), reg("k3"), reg("dst2", 36, 54), ALU.add)
        gather("V", reg("fb", 0, 96), reg("fa"), reg("o2", 0, 6))
        tt(reg("k4"), reg("s1s"), reg("d34", 18, 36), ALU.mult)
        vcopy(reg("fp1"), reg("ps1", 0, C))
        both("fa", "fb", "o3")
        tt(reg("o4"), reg("k4"), reg("dst2", 54, 72), ALU.add)
        gcopy(reg("ff1"), reg("fp1"))
        both("fb", "fa", "o4")
        both("nval", "fb", "a1")
        for a, b in XH:
            scan(reg("scn", a, b), reg("nval", a, b), reg("cm", a, b), 0.0, ALU.mult)
        for b in (2, 3):
            scopy(reg("fp%d" % b), reg("ps%d" % b, 0, C))
        table(reg("noff"), "scn")
        qz, zl = "qz%d" % r, "zl%d" % r
        for b in (2, 3):
            by_list(b)
        for b in (0, 1):
            tt(reg("yp%d" % b), reg("fp%d" % b), reg("ff%d" % b), ALU.add, reg("noff"))
        for b in (0, 1):
            gather("S", reg("zt", 512 + b, 1152, 4), reg("yp%d" % b), reg("noff", 8, 18))
        for b in (2, 3):
            vcopy(reg("gc%d" % b, 128, C), reg("gp%d" % b, 128, C))
        for b in (2, 3):
            mean(b, 128, 128, C)
        for b in (2, 3):
            scopy(reg("gc%d" % b, 0, 128), reg("gp%d" % b, 0, 128))
        for b in (0, 1):
            gather("S", reg("zt", b, 512, 4), reg("yp%d" % b), reg("noff", 0, 8))
        quant(qz, reg("zt", 512, 1152), 128, C)
        dst = T.cores[rank ^ step]
        rid, pid = topo.addr(dst, core)
        zc, zs, arr = reg(qz, HC, C), reg(qz + "s", HC, C), "arr%d" % r
        order("G", [zc, zs], [])
        g.remote_dma(T[zl][:, 0:HC].bitcast(dt.uint8), view(zc).bitcast(dt.uint8), T.sem[arr], T.sem.loc, pid, rid, use)
        g.remote_dma(T[zl + "s"][:, 0:HC], view(zs), T.sem[arr], T.sem.loc, pid, rid, use)
        count["loc"] = count.get("loc", 0) + 2 * engines
        count[arr] = 2 * engines
        clock[(arr, 2 * engines)] = {arr: 2 * engines}
        for n in (zl, zl + "s"):
            log[n] = [(reg(n), (arr, 2 * engines), "R", True)]
        if last:
            for s, v in count.items():
                if s[0] == "d":
                    wait("G", (s, v))
        if not last:
            dmas("Y", [move(reg("taf", 0, 18, 1, 16 * h, 16), reg("noff", 0, 18, 1, 16 * h - 16, 16)) for h in range(1, 8, 2)])
        rm, ri, rf = reg("mv2", 0, C), reg("iot"), reg("noff")
        op("V", lambda: g.vector.tensor_copy(view(rm).indirect(view(rf)), view(ri)), [ri, rf], [rm])
        if not last:
            dmas("Y", [move(reg("mv2", C, 2 * C, 1, 16 * h, 16), reg("mv2", 0, C, 1, 16 * h - 16, 16)) for h in range(1, 8, 2)])
        mean(2, 0, 0, 128)
        scan(reg("scn"), rm, reg("cm"), 0.0, ALU.mult)
        mean(3, 0, 0, 128)
        table(reg("moff"), "scn")
        if not last:
            table(OM, "scn")
        quant(qz, reg("zt", 0, 512), 0, 128)
        layer(qz)
        if last:
            for b in (0, 1):
                by_list(b)
            ts(reg("nlb"), reg("nval"), -1.0, None, ALU.add)
            quant("qv", reg("vin"))
            dmas("Y", [(T.nl[h:h + 1, :], view(reg("nlb", 0, C, 1, 16 * h, 1)), [reg("nlb")], []) for h in range(8)])
            heights("hta", (0,))
            unpack("qha", "hta")
            state(0, range(4))
        else:
            ts(reg("k0"), OM, "od", None, ALU.mult)
            vcopy(ON, reg("noff"))
            tt(reg("tbf"), reg("k0"), reg("tbs"), ALU.add)
            gather("S", reg("al"), reg("nval"), reg("taf"))
            gather("S", W1, reg("al"), reg("pb1"))
            by_list(0)
            own_table(AL, reg("al"), lambda: heights("hta", (0,)))
            by_list(1)
            unpack("qha", "hta")
            gather("S", reg("be"), reg("mv2"), reg("tbf"))
            own_table(GA, W1, lambda: state(0, (0,)))
            own_table(BE, reg("be"), lambda: state(0, (1,)))
            shift()
            scopy(W0, reg("al"))
            state(0, (2, 3))
        layer(zl)
        heights("htb", (0, 2))
        unpack("qhb", "htb")
        state(1, range(4))
        into_place(0)

    for k, (a, b) in enumerate(XH):
        quant("qx", reg("xtl", 4 * a, 4 * b), a, b)
        rc = reg("qx", a, b)
        dmas("Y", [(T.oc[:, 4 * a:4 * b], view(rc).bitcast(dt.uint8), [rc], [])])
        mm(4 + k, b - a, "qv", 0, "qx", a)
        if not k:
            into_place(1)
    rs = reg("qxs")
    ya, yc = reg("yb", 0, 160), reg("yb", 160, C)
    scopy(ya, reg("ps4", 0, 160))
    dmas("S", [(T.y[:, 0:160], view(ya), [ya], [])])
    vcopy(yc, reg("ps5", 0, 128))
    dmas("Y", [(T.y[:, 160:C], view(yc), [yc], [])])
    dmas("Y", [(T.osc[4 * k:4 * k + 4, :], T.qxs[32 * k:32 * k + 4, 0:C], [rs], []) for k in range(4)])
    for s, v in count.items():
        if known["G"].get(s, 0) < v:
            g.wait_ge(T.sem[s], v)
